import numpy as np
import ml_dtypes


def mxq(x, axis, fmt="e4m3"):
    dtype, down = {"e4m3": (ml_dtypes.float8_e4m3fn, 7), "e5m2": (ml_dtypes.float8_e5m2, 14)}[fmt]
    v = np.moveaxis(np.asarray(x, np.float32).astype(ml_dtypes.bfloat16).astype(np.float64), axis, -1)
    blocks = v.reshape(v.shape[:-1] + (-1, 32))
    amax = np.abs(blocks).max(-1, keepdims=True)
    byte = np.maximum(np.where(amax > 0, np.frexp(amax)[1] - 1 + 127, 0) - down, 1)
    scale = np.exp2(byte - 127.0)
    codes = (blocks / scale).astype(np.float32).astype(dtype).astype(np.float64)
    return np.moveaxis((codes * scale).reshape(v.shape), -1, axis)


WIDE = False


def mx_kscale(k):
    if not WIDE:
        return np.ones(k)
    levels = np.array([24, -24, 12, -12, 0])
    if k % 512:
        return np.exp2(np.random.permutation(np.resize(levels, k // 32))).repeat(32)
    a = np.empty((k // 512, 16))
    for p in range(k // 512):
        a[p, :8] = np.random.permutation(np.resize(levels, 8))
        for g in range(8):
            far = levels[np.abs(levels - a[p, g]) >= 10]
            a[p, g + 8] = far[np.random.randint(len(far))]
    return np.exp2(a.ravel()).repeat(32)


def f64(x):
    return np.asarray(x).astype(np.float64)


def striped(idx):
    return np.tile(idx.reshape(-1, 16).T, (8, 1)).astype(np.uint16)


def unstriped(offs):
    return offs[:16].T.reshape(-1).astype(np.int64)


E2M1 = np.array([0.0, 0.5, 1.0, 1.5, 2.0, 3.0, 4.0, 6.0, -0.0, -0.5, -1.0, -1.5, -2.0, -3.0, -4.0, -6.0])


def pack_weight(w, fmt):
    k, n = w.shape
    w = f64(np.asarray(w, np.float32).astype(ml_dtypes.bfloat16)).reshape(k // 32, 32, n)
    amax = np.abs(w).max(1)
    if fmt == "e4m3":
        byte = np.frexp(amax)[1] - 1 + 127 - 7
    else:
        mant, ex = np.frexp(amax / 6.0)
        byte = np.where(mant > 0.5, ex, ex - 1) + 127
    byte = np.clip(np.where(amax > 0, byte, 1), 1, 254)
    scaled = (w * np.exp2(127.0 - byte)[:, None, :]).reshape(k, n).astype(np.float32)
    by_word = np.ascontiguousarray(scaled.reshape(k // 512, 128, 4, n).transpose(0, 1, 3, 2))
    if fmt == "e4m3":
        words = by_word.astype(ml_dtypes.float8_e4m3fn).view(np.uint8)
    else:
        c = by_word.astype(ml_dtypes.float4_e2m1fn).view(np.uint8) & 0xF
        words = (c[..., 0::2] | (c[..., 1::2] << 4)).reshape(k // 512, 128, 2 * n)
    return np.ascontiguousarray(words), np.ascontiguousarray(byte.astype(np.uint8).reshape(k // 512, 16, n))


def unpack_weight(words, scales, fmt):
    g, _, n = scales.shape
    words = np.ascontiguousarray(words).reshape(g, 128, n, -1)
    if fmt == "e4m3":
        vals = words.view(ml_dtypes.float8_e4m3fn).astype(np.float64)
    else:
        nib = np.empty((g, 128, n, 4), np.uint8)
        nib[..., 0::2] = words & 0xF
        nib[..., 1::2] = words >> 4
        vals = E2M1[nib]
    vals = vals * np.repeat(np.exp2(scales.astype(np.float64) - 127.0), 8, axis=1)[..., None]
    return vals.transpose(0, 1, 3, 2).reshape(g * 512, n)


K, R, N, T, J = 1024, 512, 512, 2048, 1024


def setup_inputs():
    n = np.random.standard_normal
    s = mx_kscale(K)[:, None]
    u = mx_kscale(R)[:, None]
    p_tab = pack_weight(n((K, T)) * s, "e4m3")
    return {
        "tab_words": p_tab[0],
        "tab_scales": p_tab[1],
        "wu": (n((K, R)) / np.sqrt(K) / s * u.T).astype(np.float32),
        "wd": (n((R, N)) / np.sqrt(R) / u).astype(np.float32),
        "rT": (n((N, T))).astype(np.float32),
        "b": (0.3 * n(N)).astype(np.float32),
        "wgo": np.tile(np.random.uniform(0.5, 2.0, J), (128, 1)).astype(np.float32),
        "offs": striped(np.random.permutation(T)[:J]),
    }


def reference(tab_words, tab_scales, wu, wd, rT, b, wgo, offs):
    idx = unstriped(offs)
    tab_ = unpack_weight(tab_words, tab_scales, "e4m3")[:, idx]
    wu_ = mxq(f64(wu), 0, "e4m3")
    a = wu_.T @ tab_
    h = np.maximum(a, 0.0)
    h_ = mxq(h, 0, "e4m3")
    wd_ = mxq(f64(wd), 0, "e4m3")
    y = wd_.T @ h_
    out = np.zeros((N, T))
    out[:, idx] = f64(wgo)[0] * (y + f64(rT)[:, idx] + f64(b)[:, None])
    return out

@@ -1,0 +1,234 @@
+from contextlib import ExitStack
+
+import concourse.mybir as mybir
+
+K, R, N, T, J = 1024, 512, 512, 2048, 1024
+FLOPS = 2 * K * R * J + 2 * R * N * J
+
+F32 = mybir.dt.float32
+BF16 = mybir.dt.bfloat16
+I32 = mybir.dt.int32
+U32 = mybir.dt.uint32
+U16 = mybir.dt.uint16
+U8 = mybir.dt.uint8
+FP8X4 = mybir.dt.float8_e4m3fn_x4
+ACT = mybir.ActivationFunctionType
+ALU = mybir.AluOpType
+
+P = 128
+PACK = 4
+K_PASS = P * PACK
+PASSES = K // K_PASS
+BLOCKS = N // P
+CHUNK = 128
+CHUNKS = J // CHUNK
+UP_BANKS = 6
+GROUPS = ((0, 256), (256, 512), (512, 1024))
+
+
+def tile_list_modp_relu_resb_kernel(
+    tc, tab_words, tab_scales, wu, wd, rT, b, wgo, offs, out
+):
+    nc = tc.nc
+    with ExitStack() as ctx:
+        keep = ctx.enter_context(tc.tile_pool(name="keep", bufs=1))
+        psum = ctx.enter_context(tc.psum_pool(name="psum", bufs=1))
+
+        def sb(name, shape, dtype):
+            return keep.tile(shape, dtype, name=name, align_bytes=64)
+
+        offsets = keep.tile([P, J // 16], U16, name="offsets")
+        nc.sync.dma_start(offsets[:], offs)
+
+        def listed(lo, hi):
+            return offsets[:, lo // 16 : hi // 16]
+
+        table_scales = sb("table_scales", [P, T], U8)
+        nc.vector.memset(table_scales[:].bitcast(I32), 0)
+        wu_raw, table_words = [], []
+        for a in range(PASSES):
+            raw = sb("wu_raw%d" % a, [P, PACK, R], F32)
+            nc.sync.dma_start(raw[:], wu[a * K_PASS : (a + 1) * K_PASS, :].rearrange("(p j) r -> p j r", j=PACK))
+            wu_raw.append(raw)
+            if a == 0:
+                for q in range(4):
+                    nc.sync.dma_start(
+                        table_scales[32 * q : 32 * q + 4 * PASSES, :].bitcast(I32),
+                        tab_scales[:, 4 * q : 4 * q + 4, :].bitcast(I32),
+                    )
+            words = sb("table_words%d" % a, [P, T], U32)
+            nc.sync.dma_start(words[:].bitcast(I32), tab_words[a].rearrange("p t i -> p (t i)").bitcast(I32))
+            table_words.append(words)
+        bias = sb("bias", [P, BLOCKS - 1], F32)
+        bias_cols = b.rearrange("(c p) -> p c", p=P)
+        bias_first = sb("bias_first", [P, 1], F32)
+        wd_rows = wd.rearrange("(p j) n -> p j n", j=PACK)
+        wd_first = sb("wd_first", [P, PACK, P], F32)
+        nc.sync.dma_start(wd_first[:], wd_rows[:, :, :P])
+        with nc.allow_non_contiguous_dma(reason="one bias value a partition"):
+            nc.sync.dma_start(bias_first[:], bias_cols[:, :1])
+        residual = [sb("residual%d" % c, [P, T], F32) for c in range(BLOCKS)]
+        nc.sync.dma_start(residual[0][:], rT[:P, :])
+        gate = sb("gate", [P, J], F32)
+        nc.sync.dma_start(gate[:, : J // 2], wgo[:, : J // 2])
+        wd_rest = sb("wd_rest", [P, PACK, N - P], F32)
+        nc.sync.dma_start(wd_rest[:], wd_rows[:, :, P:])
+        nc.sync.dma_start(gate[:, J // 2 :], wgo[:, J // 2 :])
+        with nc.allow_non_contiguous_dma(reason="one bias value a partition"):
+            nc.sync.dma_start(bias[:], bias_cols[:, 1:])
+        for c in range(1, BLOCKS):
+            nc.sync.dma_start(residual[c][:], rT[c * P : (c + 1) * P, :])
+
+        pages = [sb("page%d" % i, [P, T], F32) for i in range(2)]
+        for page in pages:
+            nc.vector.memset(page[:], 0.0)
+
+        v_scales = sb("v_scales", [P, J], U8)
+        nc.vector.tensor_copy(v_scales[:], table_scales[:].indirect(offsets[:]))
+
+        def round_wu(engine_copy, dst, raw, m0, m1):
+            engine_copy(
+                dst[:].rearrange("p (t m j) -> p m j t", t=PACK, j=PACK)[:, m0:m1],
+                raw[:].rearrange("p j (m t) -> p m j t", t=PACK)[:, m0:m1],
+            )
+
+        def scalar_round(dst, src):
+            nc.scalar.activation(dst, src, ACT.Copy)
+
+        wu_bf = [sb("wu_bf%d" % a, [P, PACK * R], BF16) for a in range(PASSES)]
+        wu_codes = [sb("wu_codes%d" % a, [P, R], U32) for a in range(PASSES)]
+        wu_scales = [sb("wu_scales%d" % a, [P, R], U8) for a in range(PASSES)]
+        v_words = [sb("v_words%d" % a, [P, J], U32) for a in range(PASSES)]
+
+        round_wu(scalar_round, wu_bf[0], wu_raw[0], 0, P)
+        nc.vector.tensor_copy(v_words[0][:], table_words[0][:].indirect(offsets[:]))
+        nc.vector.quantize_mx(wu_codes[0][:].bitcast(FP8X4), wu_scales[0][:], wu_bf[0][:])
+        round_wu(scalar_round, wu_bf[1], wu_raw[1], 0, P // 2)
+        round_wu(nc.vector.tensor_copy, wu_bf[1], wu_raw[1], P // 2, P)
+
+        def up_pass(bank, a, chunk):
+            cols = slice(chunk * CHUNK, (chunk + 1) * CHUNK)
+            for t in range(PACK):
+                w_cols = slice(t * P, (t + 1) * P)
+                nc.tensor.matmul_mx(
+                    bank[:, t, :],
+                    lhsT=wu_codes[a][:, w_cols].bitcast(FP8X4),
+                    lhsT_scale=wu_scales[a][:, w_cols],
+                    rhs=v_words[a][:, cols].bitcast(FP8X4),
+                    rhs_scale=v_scales[4 * a :, cols],
+                    start=(a == 0 and t == 0),
+                    stop=(a == PASSES - 1 and t == PACK - 1),
+                )
+
+        def up_bank(chunk):
+            return psum.tile([P, PACK, CHUNK], F32, name="up%d" % (chunk % UP_BANKS))
+
+        banks = {}
+        for chunk in range(UP_BANKS):
+            banks[chunk] = up_bank(chunk)
+            up_pass(banks[chunk], 0, chunk)
+
+        nc.vector.quantize_mx(wu_codes[1][:].bitcast(FP8X4), wu_scales[1][:], wu_bf[1][:])
+        for lo, hi in GROUPS:
+            nc.vector.tensor_copy(v_words[1][:, lo:hi], table_words[1][:].indirect(listed(lo, hi)))
+
+        wd_bf = sb("wd_bf", [P, PACK * N], BF16)
+        wd_codes = sb("wd_codes", [P, N], U32)
+        wd_scales = sb("wd_scales", [P, N], U8)
+
+        def round_wd(raw, n0, n1):
+            scalar_round(
+                wd_bf[:, PACK * n0 : PACK * n1].rearrange("p (c i j) -> p c j i", i=4, j=PACK),
+                raw[:].rearrange("p j (c i) -> p c j i", i=4),
+            )
+
+        def quantize_wd(n0, n1):
+            nc.vector.quantize_mx(
+                wd_codes[:, n0:n1].bitcast(FP8X4), wd_scales[:, n0:n1], wd_bf[:, PACK * n0 : PACK * n1]
+            )
+
+        round_wd(wd_first, 0, P)
+        quantize_wd(0, P)
+
+        h_bf = sb("h_bf", [P, PACK * J], BF16)
+        h_codes = sb("h_codes", [P, J], U32)
+        h_scales = sb("h_scales", [P, J], U8)
+
+        def finish_up(lo, hi):
+            for chunk in range(lo // CHUNK, hi // CHUNK):
+                if chunk not in banks:
+                    banks[chunk] = up_bank(chunk)
+                    up_pass(banks[chunk], 0, chunk)
+                up_pass(banks[chunk], 1, chunk)
+                nc.scalar.activation(
+                    h_bf[:, PACK * CHUNK * chunk : PACK * CHUNK * (chunk + 1)].rearrange("p (n t) -> p n t", t=PACK),
+                    banks[chunk][:].rearrange("p t n -> p n t"),
+                    ACT.Relu,
+                )
+
+        def quantize_h(lo, hi):
+            nc.vector.quantize_mx(
+                h_codes[:, lo:hi].bitcast(FP8X4), h_scales[:, lo:hi], h_bf[:, PACK * lo : PACK * hi]
+            )
+
+        y_bias = [sb("y_bias%d" % c, [P, J], F32) for c in range(BLOCKS)]
+        summed = [sb("summed%d" % c, [P, J], F32) for c in range(BLOCKS)]
+        down_count = []
+
+        def down(c, lo, hi):
+            bank = psum.tile([P, 512], F32, name="down%d" % (len(down_count) % 2))
+            down_count.append(c)
+            n_cols = slice(c * P, (c + 1) * P)
+            nc.tensor.matmul_mx(
+                bank[:, : hi - lo],
+                lhsT=wd_codes[:, n_cols].bitcast(FP8X4),
+                lhsT_scale=wd_scales[:, n_cols],
+                rhs=h_codes[:, lo:hi].bitcast(FP8X4),
+                rhs_scale=h_scales[:, lo:hi],
+                start=True,
+                stop=True,
+            )
+            nc.scalar.activation(y_bias[c][:, lo:hi], bank[:, : hi - lo], ACT.Identity, bias=(bias_first[:] if c == 0 else bias[:, c - 1 : c]))
+
+        def add_residual(c, lo, hi):
+            nc.vector.tensor_tensor(
+                summed[c][:, lo:hi], residual[c][:].indirect(listed(lo, hi)), y_bias[c][:, lo:hi], ALU.add
+            )
+
+        def place(c, lo, hi):
+            nc.vector.tensor_tensor(
+                pages[c % 2][:].indirect(listed(lo, hi)), summed[c][:, lo:hi], gate[:, lo:hi], ALU.mult
+            )
+
+        def store(c):
+            nc.sync.dma_start(out[c * P : (c + 1) * P, :], pages[c % 2][:])
+
+        g0, g1, g2 = GROUPS
+        finish_up(*g0)
+        quantize_h(*g0)
+        down(0, *g0)
+        finish_up(*g1)
+        add_residual(0, *g0)
+        quantize_h(*g1)
+        down(0, *g1)
+        finish_up(*g2)
+        place(0, *g0)
+        add_residual(0, *g1)
+        quantize_h(*g2)
+        down(0, *g2)
+        round_wd(wd_rest, P, N)
+        place(0, *g1)
+        add_residual(0, *g2)
+        quantize_wd(P, 2 * P)
+        quantize_wd(2 * P, N)
+        for c in range(1, BLOCKS):
+            down(c, 0, J // 2)
+            down(c, J // 2, J)
+        pending = g2
+        for c in range(1, BLOCKS):
+            add_residual(c, 0, J)
+            place(c - 1, *pending)
+            store(c - 1)
+            pending = (0, J)
+        place(BLOCKS - 1, 0, J)
+        store(BLOCKS - 1)

@@ -24,6 +24,7 @@ CHUNK = 128
 CHUNKS = J // CHUNK
 UP_BANKS = 6
 GROUPS = ((0, 256), (256, 512), (512, 1024))
+HALVES = ((0, 512), (512, 1024))
 
 
 def tile_list_modp_relu_resb_kernel(
@@ -34,8 +35,8 @@ def tile_list_modp_relu_resb_kernel(
         keep = ctx.enter_context(tc.tile_pool(name="keep", bufs=1))
         psum = ctx.enter_context(tc.psum_pool(name="psum", bufs=1))
 
-        def sb(name, shape, dtype):
-            return keep.tile(shape, dtype, name=name, align_bytes=64)
+        def sb(name, shape, dtype, on=None):
+            return keep.tile(shape, dtype, name=name, tag=on or name, align_bytes=64)
 
         offsets = keep.tile([P, J // 16], U16, name="offsets")
         nc.sync.dma_start(offsets[:], offs)
@@ -44,67 +45,70 @@ def tile_list_modp_relu_resb_kernel(
             return offsets[:, lo // 16 : hi // 16]
 
         table_scales = sb("table_scales", [P, T], U8)
-        nc.vector.memset(table_scales[:].bitcast(I32), 0)
+        nc.gpsimd.memset(table_scales[:].bitcast(I32), 0)
+        for q in range(4):
+            nc.sync.dma_start(
+                table_scales[32 * q : 32 * q + 4 * PASSES, :].bitcast(I32),
+                tab_scales[:, 4 * q : 4 * q + 4, :].bitcast(I32),
+            )
         wu_raw, table_words = [], []
         for a in range(PASSES):
-            raw = sb("wu_raw%d" % a, [P, PACK, R], F32)
-            nc.sync.dma_start(raw[:], wu[a * K_PASS : (a + 1) * K_PASS, :].rearrange("(p j) r -> p j r", j=PACK))
-            wu_raw.append(raw)
-            if a == 0:
-                for q in range(4):
-                    nc.sync.dma_start(
-                        table_scales[32 * q : 32 * q + 4 * PASSES, :].bitcast(I32),
-                        tab_scales[:, 4 * q : 4 * q + 4, :].bitcast(I32),
-                    )
+            rows = wu[a * K_PASS : (a + 1) * K_PASS, :].rearrange("(p j) r -> p j r", j=PACK)
+            width = R // (a + 1)
+            for r0 in range(0, R, width):
+                raw = sb("wu_raw%d_%d" % (a, r0), [P, PACK, width], F32)
+                nc.sync.dma_start(raw[:], rows[:, :, r0 : r0 + width])
+                wu_raw.append(raw)
             words = sb("table_words%d" % a, [P, T], U32)
             nc.sync.dma_start(words[:].bitcast(I32), tab_words[a].rearrange("p t i -> p (t i)").bitcast(I32))
             table_words.append(words)
-        bias = sb("bias", [P, BLOCKS - 1], F32)
         bias_cols = b.rearrange("(c p) -> p c", p=P)
         bias_first = sb("bias_first", [P, 1], F32)
+        bias_rest = sb("bias_rest", [P, BLOCKS - 1], F32)
         wd_rows = wd.rearrange("(p j) n -> p j n", j=PACK)
         wd_first = sb("wd_first", [P, PACK, P], F32)
         nc.sync.dma_start(wd_first[:], wd_rows[:, :, :P])
-        with nc.allow_non_contiguous_dma(reason="one bias value a partition"):
-            nc.sync.dma_start(bias_first[:], bias_cols[:, :1])
         residual = [sb("residual%d" % c, [P, T], F32) for c in range(BLOCKS)]
         nc.sync.dma_start(residual[0][:], rT[:P, :])
+        with nc.allow_non_contiguous_dma(reason="one bias value a partition"):
+            nc.sync.dma_start(bias_first[:], bias_cols[:, :1])
         gate = sb("gate", [P, J], F32)
         nc.sync.dma_start(gate[:, : J // 2], wgo[:, : J // 2])
         wd_rest = sb("wd_rest", [P, PACK, N - P], F32)
         nc.sync.dma_start(wd_rest[:], wd_rows[:, :, P:])
         nc.sync.dma_start(gate[:, J // 2 :], wgo[:, J // 2 :])
         with nc.allow_non_contiguous_dma(reason="one bias value a partition"):
-            nc.sync.dma_start(bias[:], bias_cols[:, 1:])
+            nc.sync.dma_start(bias_rest[:], bias_cols[:, 1:])
         for c in range(1, BLOCKS):
             nc.sync.dma_start(residual[c][:], rT[c * P : (c + 1) * P, :])
 
         pages = [sb("page%d" % i, [P, T], F32) for i in range(2)]
-        for page in pages:
-            nc.vector.memset(page[:], 0.0)
+        nc.vector.memset(pages[0][:], 0.0)
+        nc.gpsimd.memset(pages[1][:], 0.0)
 
         v_scales = sb("v_scales", [P, J], U8)
         nc.vector.tensor_copy(v_scales[:], table_scales[:].indirect(offsets[:]))
 
-        def round_wu(engine_copy, dst, raw, m0, m1):
-            engine_copy(
-                dst[:].rearrange("p (t m j) -> p m j t", t=PACK, j=PACK)[:, m0:m1],
-                raw[:].rearrange("p j (m t) -> p m j t", t=PACK)[:, m0:m1],
-            )
-
         def scalar_round(dst, src):
             nc.scalar.activation(dst, src, ACT.Copy)
+
+        def round_wu(dst, raw, m0, m1):
+            scalar_round(
+                dst[:].rearrange("p (t m j) -> p m j t", t=PACK, j=PACK)[:, m0:m1],
+                raw[:].rearrange("p j (m t) -> p m j t", t=PACK),
+            )
 
         wu_bf = [sb("wu_bf%d" % a, [P, PACK * R], BF16) for a in range(PASSES)]
         wu_codes = [sb("wu_codes%d" % a, [P, R], U32) for a in range(PASSES)]
         wu_scales = [sb("wu_scales%d" % a, [P, R], U8) for a in range(PASSES)]
         v_words = [sb("v_words%d" % a, [P, J], U32) for a in range(PASSES)]
 
-        round_wu(scalar_round, wu_bf[0], wu_raw[0], 0, P)
-        nc.vector.tensor_copy(v_words[0][:], table_words[0][:].indirect(offsets[:]))
+        round_wu(wu_bf[0], wu_raw[0], 0, P)
         nc.vector.quantize_mx(wu_codes[0][:].bitcast(FP8X4), wu_scales[0][:], wu_bf[0][:])
-        round_wu(scalar_round, wu_bf[1], wu_raw[1], 0, P // 2)
-        round_wu(nc.vector.tensor_copy, wu_bf[1], wu_raw[1], P // 2, P)
+        for lo in (0, J // 2):
+            nc.vector.tensor_copy(v_words[0][:, lo : lo + J // 2], table_words[0][:].indirect(listed(lo, lo + J // 2)))
+        round_wu(wu_bf[1], wu_raw[1], 0, P // 2)
+        round_wu(wu_bf[1], wu_raw[2], P // 2, P)
 
         def up_pass(bank, a, chunk):
             cols = slice(chunk * CHUNK, (chunk + 1) * CHUNK)
@@ -132,26 +136,27 @@ def tile_list_modp_relu_resb_kernel(
         for lo, hi in GROUPS:
             nc.vector.tensor_copy(v_words[1][:, lo:hi], table_words[1][:].indirect(listed(lo, hi)))
 
-        wd_bf = sb("wd_bf", [P, PACK * N], BF16)
         wd_codes = sb("wd_codes", [P, N], U32)
         wd_scales = sb("wd_scales", [P, N], U8)
 
-        def round_wd(raw, n0, n1):
+        def round_wd(name, raw, width):
+            rounded = sb(name, [P, PACK * width], BF16)
             scalar_round(
-                wd_bf[:, PACK * n0 : PACK * n1].rearrange("p (c i j) -> p c j i", i=4, j=PACK),
+                rounded[:].rearrange("p (c i j) -> p c j i", i=4, j=PACK),
                 raw[:].rearrange("p j (c i) -> p c j i", i=4),
             )
+            return rounded
 
-        def quantize_wd(n0, n1):
-            nc.vector.quantize_mx(
-                wd_codes[:, n0:n1].bitcast(FP8X4), wd_scales[:, n0:n1], wd_bf[:, PACK * n0 : PACK * n1]
-            )
+        def quantize_wd(n0, n1, rounded):
+            nc.vector.quantize_mx(wd_codes[:, n0:n1].bitcast(FP8X4), wd_scales[:, n0:n1], rounded)
 
-        round_wd(wd_first, 0, P)
-        quantize_wd(0, P)
+        quantize_wd(0, P, round_wd("wd_first_bf", wd_first, P)[:])
 
-        h_bf = sb("h_bf", [P, PACK * J], BF16)
-        h_codes = sb("h_codes", [P, J], U32)
+        picked = sb("picked", [P, J], F32)
+        nc.vector.tensor_copy(picked[:], residual[0][:].indirect(offsets[:]))
+
+        h_bf = {lo: sb("h_bf%d" % lo, [P, PACK * (hi - lo)], BF16, on=None if lo else "wd_first") for lo, hi in HALVES}
+        h_codes = sb("h_codes", [P, J], U32, on="residual0")
         h_scales = sb("h_scales", [P, J], U8)
 
         def finish_up(lo, hi):
@@ -160,19 +165,18 @@ def tile_list_modp_relu_resb_kernel(
                     banks[chunk] = up_bank(chunk)
                     up_pass(banks[chunk], 0, chunk)
                 up_pass(banks[chunk], 1, chunk)
+                at = PACK * (CHUNK * chunk - lo)
                 nc.scalar.activation(
-                    h_bf[:, PACK * CHUNK * chunk : PACK * CHUNK * (chunk + 1)].rearrange("p (n t) -> p n t", t=PACK),
+                    h_bf[lo][:, at : at + PACK * CHUNK].rearrange("p (n t) -> p n t", t=PACK),
                     banks[chunk][:].rearrange("p t n -> p n t"),
                     ACT.Relu,
                 )
 
         def quantize_h(lo, hi):
-            nc.vector.quantize_mx(
-                h_codes[:, lo:hi].bitcast(FP8X4), h_scales[:, lo:hi], h_bf[:, PACK * lo : PACK * hi]
-            )
+            nc.vector.quantize_mx(h_codes[:, lo:hi].bitcast(FP8X4), h_scales[:, lo:hi], h_bf[lo][:])
 
-        y_bias = [sb("y_bias%d" % c, [P, J], F32) for c in range(BLOCKS)]
-        summed = [sb("summed%d" % c, [P, J], F32) for c in range(BLOCKS)]
+        y_bias = {c: sb("y_bias%d" % c, [P, J], F32) for c in range(1, BLOCKS)}
+        summed = {c: sb("summed%d" % c, [P, J], F32) for c in range(1, BLOCKS)}
         down_count = []
 
         def down(c, lo, hi):
@@ -188,47 +192,48 @@ def tile_list_modp_relu_resb_kernel(
                 start=True,
                 stop=True,
             )
-            nc.scalar.activation(y_bias[c][:, lo:hi], bank[:, : hi - lo], ACT.Identity, bias=(bias_first[:] if c == 0 else bias[:, c - 1 : c]))
+            return bank[:, : hi - lo]
 
-        def add_residual(c, lo, hi):
-            nc.vector.tensor_tensor(
-                summed[c][:, lo:hi], residual[c][:].indirect(listed(lo, hi)), y_bias[c][:, lo:hi], ALU.add
-            )
+        def bias_of(c):
+            return bias_rest[:, c - 1 : c] if c else bias_first[:]
 
-        def place(c, lo, hi):
-            nc.vector.tensor_tensor(
-                pages[c % 2][:].indirect(listed(lo, hi)), summed[c][:, lo:hi], gate[:, lo:hi], ALU.mult
-            )
+        def down_bias(c, lo, hi):
+            nc.scalar.activation(y_bias[c][:, lo:hi], down(c, lo, hi), ACT.Identity, bias=bias_of(c))
+
+        def sum_from_bank(lo, hi, on):
+            total = sb("summed0_%d" % lo, [P, hi - lo], F32, on=on)
+            nc.vector.scalar_tensor_tensor(total[:], down(0, lo, hi), bias_of(0), picked[:, lo:hi], ALU.add, ALU.add)
+            return total
+
+        def add_residual(c):
+            nc.vector.tensor_tensor(summed[c][:], residual[c][:].indirect(offsets[:]), y_bias[c][:], ALU.add)
+
+        def place(c, lo, hi, values):
+            nc.vector.tensor_tensor(pages[c % 2][:].indirect(listed(lo, hi)), values[:], gate[:, lo:hi], ALU.mult)
 
         def store(c):
             nc.sync.dma_start(out[c * P : (c + 1) * P, :], pages[c % 2][:])
 
-        g0, g1, g2 = GROUPS
-        finish_up(*g0)
-        quantize_h(*g0)
-        down(0, *g0)
-        finish_up(*g1)
-        add_residual(0, *g0)
-        quantize_h(*g1)
-        down(0, *g1)
-        finish_up(*g2)
-        place(0, *g0)
-        add_residual(0, *g1)
-        quantize_h(*g2)
-        down(0, *g2)
-        round_wd(wd_rest, P, N)
-        place(0, *g1)
-        add_residual(0, *g2)
-        quantize_wd(P, 2 * P)
-        quantize_wd(2 * P, N)
+        first, second = HALVES
+        finish_up(*first)
+        quantize_h(*first)
+        finish_up(*second)
+        quantize_h(*second)
+        total0 = sum_from_bank(*first, "h_bf%d" % second[0])
+        wd_rest_bf = round_wd("wd_rest_bf", wd_rest, N - P)
+        place(0, *first, total0)
+        quantize_wd(P, 2 * P, wd_rest_bf[:, : PACK * P])
+        quantize_wd(2 * P, N, wd_rest_bf[:, PACK * P :])
+        total1 = sum_from_bank(*second, "wd_rest_bf")
         for c in range(1, BLOCKS):
-            down(c, 0, J // 2)
-            down(c, J // 2, J)
-        pending = g2
-        for c in range(1, BLOCKS):
-            add_residual(c, 0, J)
-            place(c - 1, *pending)
+            down_bias(c, 0, J // 2)
+            down_bias(c, J // 2, J)
+        place(0, *second, total1)
+        store(0)
+        add_residual(1)
+        for c in range(2, BLOCKS):
+            add_residual(c)
+            place(c - 1, 0, J, summed[c - 1])
             store(c - 1)
-            pending = (0, J)
-        place(BLOCKS - 1, 0, J)
+        place(BLOCKS - 1, 0, J, summed[BLOCKS - 1])
         store(BLOCKS - 1)

@@ -22,9 +22,8 @@ PASSES = K // K_PASS
 BLOCKS = N // P
 CHUNK = 128
 CHUNKS = J // CHUNK
-UP_BANKS = 6
+BANKS = 8
 GROUPS = ((0, 256), (256, 512), (512, 1024))
-HALVES = ((0, 512), (512, 1024))
 
 
 def tile_list_modp_relu_resb_kernel(
@@ -44,6 +43,8 @@ def tile_list_modp_relu_resb_kernel(
         def listed(lo, hi):
             return offsets[:, lo // 16 : hi // 16]
 
+        bias_rows = sb("bias_rows", [P, BLOCKS * 32], F32)
+        nc.gpsimd.memset(bias_rows[:], 0.0)
         table_scales = sb("table_scales", [P, T], U8)
         nc.gpsimd.memset(table_scales[:].bitcast(I32), 0)
         for q in range(4):
@@ -51,35 +52,35 @@ def tile_list_modp_relu_resb_kernel(
                 table_scales[32 * q : 32 * q + 4 * PASSES, :].bitcast(I32),
                 tab_scales[:, 4 * q : 4 * q + 4, :].bitcast(I32),
             )
+        nc.sync.dma_start(
+            bias_rows[0:P:32, :].rearrange("q (c i) -> q c i", i=32), b.rearrange("(c q i) -> q c i", q=4, i=32)
+        )
         wu_raw, table_words = [], []
         for a in range(PASSES):
-            rows = wu[a * K_PASS : (a + 1) * K_PASS, :].rearrange("(p j) r -> p j r", j=PACK)
-            width = R // (a + 1)
-            for r0 in range(0, R, width):
-                raw = sb("wu_raw%d_%d" % (a, r0), [P, PACK, width], F32)
-                nc.sync.dma_start(raw[:], rows[:, :, r0 : r0 + width])
-                wu_raw.append(raw)
+            raw = sb("wu_raw%d" % a, [P, PACK, R], F32)
+            nc.sync.dma_start(raw[:], wu[a * K_PASS : (a + 1) * K_PASS, :].rearrange("(p j) r -> p j r", j=PACK))
+            wu_raw.append(raw)
             words = sb("table_words%d" % a, [P, T], U32)
             nc.sync.dma_start(words[:].bitcast(I32), tab_words[a].rearrange("p t i -> p (t i)").bitcast(I32))
             table_words.append(words)
-        bias_cols = b.rearrange("(c p) -> p c", p=P)
-        bias_first = sb("bias_first", [P, 1], F32)
-        bias_rest = sb("bias_rest", [P, BLOCKS - 1], F32)
+        first, second, third = GROUPS
         wd_rows = wd.rearrange("(p j) n -> p j n", j=PACK)
         wd_first = sb("wd_first", [P, PACK, P], F32)
         nc.sync.dma_start(wd_first[:], wd_rows[:, :, :P])
         residual = [sb("residual%d" % c, [P, T], F32) for c in range(BLOCKS)]
         nc.sync.dma_start(residual[0][:], rT[:P, :])
-        with nc.allow_non_contiguous_dma(reason="one bias value a partition"):
-            nc.sync.dma_start(bias_first[:], bias_cols[:, :1])
         gate = sb("gate", [P, J], F32)
-        nc.sync.dma_start(gate[:, : J // 2], wgo[:, : J // 2])
+
+        def load_gate(lo, hi):
+            nc.sync.dma_start(gate[:, lo:hi], wgo[:, lo:hi])
+
+        load_gate(*first)
         wd_rest = sb("wd_rest", [P, PACK, N - P], F32)
         nc.sync.dma_start(wd_rest[:], wd_rows[:, :, P:])
-        nc.sync.dma_start(gate[:, J // 2 :], wgo[:, J // 2 :])
-        with nc.allow_non_contiguous_dma(reason="one bias value a partition"):
-            nc.sync.dma_start(bias_rest[:], bias_cols[:, 1:])
-        for c in range(1, BLOCKS):
+        load_gate(*second)
+        nc.sync.dma_start(residual[1][:], rT[P : 2 * P, :])
+        load_gate(*third)
+        for c in range(2, BLOCKS):
             nc.sync.dma_start(residual[c][:], rT[c * P : (c + 1) * P, :])
 
         pages = [sb("page%d" % i, [P, T], F32) for i in range(2)]
@@ -89,26 +90,26 @@ def tile_list_modp_relu_resb_kernel(
         v_scales = sb("v_scales", [P, J], U8)
         nc.vector.tensor_copy(v_scales[:], table_scales[:].indirect(offsets[:]))
 
+        bias_cols = sb("bias_cols", [P, BLOCKS * 32], F32)
+        nc.vector.transpose(bias_cols[:], bias_rows[:])
+
         def scalar_round(dst, src):
             nc.scalar.activation(dst, src, ACT.Copy)
 
-        def round_wu(dst, raw, m0, m1):
-            scalar_round(
-                dst[:].rearrange("p (t m j) -> p m j t", t=PACK, j=PACK)[:, m0:m1],
-                raw[:].rearrange("p j (m t) -> p m j t", t=PACK),
-            )
-
-        wu_bf = [sb("wu_bf%d" % a, [P, PACK * R], BF16) for a in range(PASSES)]
         wu_codes = [sb("wu_codes%d" % a, [P, R], U32) for a in range(PASSES)]
         wu_scales = [sb("wu_scales%d" % a, [P, R], U8) for a in range(PASSES)]
         v_words = [sb("v_words%d" % a, [P, J], U32) for a in range(PASSES)]
 
-        round_wu(wu_bf[0], wu_raw[0], 0, P)
-        nc.vector.quantize_mx(wu_codes[0][:].bitcast(FP8X4), wu_scales[0][:], wu_bf[0][:])
-        for lo in (0, J // 2):
-            nc.vector.tensor_copy(v_words[0][:, lo : lo + J // 2], table_words[0][:].indirect(listed(lo, lo + J // 2)))
-        round_wu(wu_bf[1], wu_raw[1], 0, P // 2)
-        round_wu(wu_bf[1], wu_raw[2], P // 2, P)
+        def quantize_wu(a):
+            rounded = [sb("wu_bf%d_%d" % (a, half), [P, 2 * R], BF16) for half in range(2)]
+            for half, copy in enumerate((nc.vector.tensor_copy, scalar_round)):
+                copy(
+                    rounded[half][:].rearrange("p (t m j) -> p m j t", t=2, j=PACK),
+                    wu_raw[a][:].rearrange("p j (m t) -> p m j t", t=PACK)[:, :, :, 2 * half : 2 * half + 2],
+                )
+            for half in range(2):
+                cols = slice(2 * P * half, 2 * P * (half + 1))
+                nc.vector.quantize_mx(wu_codes[a][:, cols].bitcast(FP8X4), wu_scales[a][:, cols], rounded[half][:])
 
         def up_pass(bank, a, chunk):
             cols = slice(chunk * CHUNK, (chunk + 1) * CHUNK)
@@ -124,20 +125,15 @@ def tile_list_modp_relu_resb_kernel(
                     stop=(a == PASSES - 1 and t == PACK - 1),
                 )
 
-        def up_bank(chunk):
-            return psum.tile([P, PACK, CHUNK], F32, name="up%d" % (chunk % UP_BANKS))
-
-        banks = {}
-        for chunk in range(UP_BANKS):
-            banks[chunk] = up_bank(chunk)
-            up_pass(banks[chunk], 0, chunk)
-
-        nc.vector.quantize_mx(wu_codes[1][:].bitcast(FP8X4), wu_scales[1][:], wu_bf[1][:])
+        quantize_wu(0)
         for lo, hi in GROUPS:
-            nc.vector.tensor_copy(v_words[1][:, lo:hi], table_words[1][:].indirect(listed(lo, hi)))
-
-        wd_codes = sb("wd_codes", [P, N], U32)
-        wd_scales = sb("wd_scales", [P, N], U8)
+            nc.vector.tensor_copy(v_words[0][:, lo:hi], table_words[0][:].indirect(listed(lo, hi)))
+        banks = [psum.tile([P, PACK, CHUNK], F32, name="bank%d" % chunk) for chunk in range(CHUNKS)]
+        for chunk in range(CHUNKS):
+            up_pass(banks[chunk], 0, chunk)
+        quantize_wu(1)
+        for lo in range(0, J, 256):
+            nc.vector.tensor_copy(v_words[1][:, lo : lo + 256], table_words[1][:].indirect(listed(lo, lo + 256)))
 
         def round_wd(name, raw, width):
             rounded = sb(name, [P, PACK * width], BF16)
@@ -147,23 +143,23 @@ def tile_list_modp_relu_resb_kernel(
             )
             return rounded
 
-        def quantize_wd(n0, n1, rounded):
-            nc.vector.quantize_mx(wd_codes[:, n0:n1].bitcast(FP8X4), wd_scales[:, n0:n1], rounded)
+        wd_codes, wd_scales = {}, {}
 
-        quantize_wd(0, P, round_wd("wd_first_bf", wd_first, P)[:])
+        def quantize_wd(c0, c1, rounded, on=None):
+            codes = sb("wd_codes%d" % c0, [P, (c1 - c0) * P], U32, on=on)
+            scales = sb("wd_scales%d" % c0, [P, (c1 - c0) * P], U8)
+            nc.vector.quantize_mx(codes[:].bitcast(FP8X4), scales[:], rounded)
+            for c in range(c0, c1):
+                wd_codes[c] = codes[:, (c - c0) * P : (c - c0 + 1) * P]
+                wd_scales[c] = scales[:, (c - c0) * P : (c - c0 + 1) * P]
 
-        picked = sb("picked", [P, J], F32)
-        nc.vector.tensor_copy(picked[:], residual[0][:].indirect(offsets[:]))
+        quantize_wd(0, 1, round_wd("wd_first_bf", wd_first, P)[:])
 
-        h_bf = {lo: sb("h_bf%d" % lo, [P, PACK * (hi - lo)], BF16, on=None if lo else "wd_first") for lo, hi in HALVES}
-        h_codes = sb("h_codes", [P, J], U32, on="residual0")
-        h_scales = sb("h_scales", [P, J], U8)
+        h_bf = {lo: sb("h_bf%d" % lo, [P, PACK * (hi - lo)], BF16, on=None if lo else "wd_first") for lo, hi in GROUPS}
+        h_codes, h_scales = {}, {}
 
         def finish_up(lo, hi):
             for chunk in range(lo // CHUNK, hi // CHUNK):
-                if chunk not in banks:
-                    banks[chunk] = up_bank(chunk)
-                    up_pass(banks[chunk], 0, chunk)
                 up_pass(banks[chunk], 1, chunk)
                 at = PACK * (CHUNK * chunk - lo)
                 nc.scalar.activation(
@@ -172,41 +168,40 @@ def tile_list_modp_relu_resb_kernel(
                     ACT.Relu,
                 )
 
-        def quantize_h(lo, hi):
-            nc.vector.quantize_mx(h_codes[:, lo:hi].bitcast(FP8X4), h_scales[:, lo:hi], h_bf[lo][:])
+        def quantize_h(lo, hi, on=None):
+            h_codes[lo] = sb("h_codes%d" % lo, [P, hi - lo], U32, on=on)
+            h_scales[lo] = sb("h_scales%d" % lo, [P, hi - lo], U8)
+            nc.vector.quantize_mx(h_codes[lo][:].bitcast(FP8X4), h_scales[lo][:], h_bf[lo][:])
 
-        y_bias = {c: sb("y_bias%d" % c, [P, J], F32) for c in range(1, BLOCKS)}
-        summed = {c: sb("summed%d" % c, [P, J], F32) for c in range(1, BLOCKS)}
         down_count = []
 
-        def down(c, lo, hi):
-            bank = psum.tile([P, 512], F32, name="down%d" % (len(down_count) % 2))
+        def down(c, groups):
+            bank = psum.tile([P, 512], F32, name="bank%d" % (len(down_count) % BANKS))
             down_count.append(c)
-            n_cols = slice(c * P, (c + 1) * P)
-            nc.tensor.matmul_mx(
-                bank[:, : hi - lo],
-                lhsT=wd_codes[:, n_cols].bitcast(FP8X4),
-                lhsT_scale=wd_scales[:, n_cols],
-                rhs=h_codes[:, lo:hi].bitcast(FP8X4),
-                rhs_scale=h_scales[:, lo:hi],
-                start=True,
-                stop=True,
-            )
-            return bank[:, : hi - lo]
+            at = 0
+            for lo, hi in groups:
+                nc.tensor.matmul_mx(
+                    bank[:, at : at + hi - lo],
+                    lhsT=wd_codes[c].bitcast(FP8X4),
+                    lhsT_scale=wd_scales[c],
+                    rhs=h_codes[lo][:].bitcast(FP8X4),
+                    rhs_scale=h_scales[lo][:],
+                    start=True,
+                    stop=True,
+                )
+                at = at + hi - lo
+            return bank[:, :at]
 
         def bias_of(c):
-            return bias_rest[:, c - 1 : c] if c else bias_first[:]
+            return bias_cols[:, 32 * c : 32 * c + 1]
 
-        def down_bias(c, lo, hi):
-            nc.scalar.activation(y_bias[c][:, lo:hi], down(c, lo, hi), ACT.Identity, bias=bias_of(c))
+        def add_bias(dst, c, groups):
+            nc.scalar.activation(dst, down(c, groups), ACT.Identity, bias=bias_of(c))
 
-        def sum_from_bank(lo, hi, on):
-            total = sb("summed0_%d" % lo, [P, hi - lo], F32, on=on)
-            nc.vector.scalar_tensor_tensor(total[:], down(0, lo, hi), bias_of(0), picked[:, lo:hi], ALU.add, ALU.add)
+        def add_residual(c, lo, hi, y):
+            total = sb("total%d_%d" % (c, lo), [P, hi - lo], F32)
+            nc.vector.tensor_tensor(total[:], residual[c][:].indirect(listed(lo, hi)), y[:], ALU.add)
             return total
-
-        def add_residual(c):
-            nc.vector.tensor_tensor(summed[c][:], residual[c][:].indirect(offsets[:]), y_bias[c][:], ALU.add)
 
         def place(c, lo, hi, values):
             nc.vector.tensor_tensor(pages[c % 2][:].indirect(listed(lo, hi)), values[:], gate[:, lo:hi], ALU.mult)
@@ -214,26 +209,40 @@ def tile_list_modp_relu_resb_kernel(
         def store(c):
             nc.sync.dma_start(out[c * P : (c + 1) * P, :], pages[c % 2][:])
 
-        first, second = HALVES
+        def pick(lo, hi):
+            picked = sb("picked%d" % lo, [P, hi - lo], F32)
+            nc.vector.tensor_copy(picked[:], residual[0][:].indirect(listed(lo, hi)))
+            return picked
+
+        def sum_from_bank(lo, hi, picked, on=None):
+            total = sb("total0_%d" % lo, [P, hi - lo], F32, on=on)
+            nc.vector.scalar_tensor_tensor(total[:], down(0, [(lo, hi)]), bias_of(0), picked[:], ALU.add, ALU.add)
+            return total
+
         finish_up(*first)
         quantize_h(*first)
+        picked_first, picked_second = pick(*first), pick(*second)
+        total_first = sum_from_bank(*first, picked_first)
         finish_up(*second)
         quantize_h(*second)
-        total0 = sum_from_bank(*first, "h_bf%d" % second[0])
+        place(0, *first, total_first)
+        total_second = sum_from_bank(*second, picked_second)
+        finish_up(*third)
+        quantize_h(*third)
+        place(0, *second, total_second)
         wd_rest_bf = round_wd("wd_rest_bf", wd_rest, N - P)
-        place(0, *first, total0)
-        quantize_wd(P, 2 * P, wd_rest_bf[:, : PACK * P])
-        quantize_wd(2 * P, N, wd_rest_bf[:, PACK * P :])
-        total1 = sum_from_bank(*second, "wd_rest_bf")
+        quantize_wd(1, 2, wd_rest_bf[:, : PACK * P])
+        quantize_wd(2, BLOCKS, wd_rest_bf[:, PACK * P :])
+        y_third = sb("y_third", [P, third[1] - third[0]], F32)
+        add_bias(y_third[:], 0, [third])
+        waiting = (third, add_residual(0, *third, y_third))
         for c in range(1, BLOCKS):
-            down_bias(c, 0, J // 2)
-            down_bias(c, J // 2, J)
-        place(0, *second, total1)
-        store(0)
-        add_residual(1)
-        for c in range(2, BLOCKS):
-            add_residual(c)
-            place(c - 1, 0, J, summed[c - 1])
+            y = sb("y%d" % c, [P, J], F32)
+            add_bias(y[:, : J // 2], c, [first, second])
+            add_bias(y[:, J // 2 :], c, [third])
+            total = add_residual(c, 0, J, y)
+            place(c - 1, *waiting[0], waiting[1])
             store(c - 1)
-        place(BLOCKS - 1, 0, J, summed[BLOCKS - 1])
+            waiting = ((0, J), total)
+        place(BLOCKS - 1, *waiting[0], waiting[1])
         store(BLOCKS - 1)

@@ -45,24 +45,29 @@ def tile_list_modp_relu_resb_kernel(
 
         bias_rows = sb("bias_rows", [P, BLOCKS * 32], F32)
         nc.gpsimd.memset(bias_rows[:], 0.0)
+        nc.sync.dma_start(
+            bias_rows[0:P:32, :].rearrange("q (c i) -> q c i", i=32), b.rearrange("(c q i) -> q c i", q=4, i=32)
+        )
         table_scales = sb("table_scales", [P, T], U8)
         nc.gpsimd.memset(table_scales[:].bitcast(I32), 0)
+        wu_raw = [sb("wu_raw%d" % a, [P, PACK, R], F32) for a in range(PASSES)]
+        table_words = [sb("table_words%d" % a, [P, T], U32) for a in range(PASSES)]
+
+        def load_wu(a):
+            nc.sync.dma_start(wu_raw[a][:], wu[a * K_PASS : (a + 1) * K_PASS, :].rearrange("(p j) r -> p j r", j=PACK))
+
+        def load_words(a):
+            nc.sync.dma_start(table_words[a][:].bitcast(I32), tab_words[a].rearrange("p t i -> p (t i)").bitcast(I32))
+
         for q in range(4):
             nc.sync.dma_start(
                 table_scales[32 * q : 32 * q + 4 * PASSES, :].bitcast(I32),
                 tab_scales[:, 4 * q : 4 * q + 4, :].bitcast(I32),
             )
-        nc.sync.dma_start(
-            bias_rows[0:P:32, :].rearrange("q (c i) -> q c i", i=32), b.rearrange("(c q i) -> q c i", q=4, i=32)
-        )
-        wu_raw, table_words = [], []
-        for a in range(PASSES):
-            raw = sb("wu_raw%d" % a, [P, PACK, R], F32)
-            nc.sync.dma_start(raw[:], wu[a * K_PASS : (a + 1) * K_PASS, :].rearrange("(p j) r -> p j r", j=PACK))
-            wu_raw.append(raw)
-            words = sb("table_words%d" % a, [P, T], U32)
-            nc.sync.dma_start(words[:].bitcast(I32), tab_words[a].rearrange("p t i -> p (t i)").bitcast(I32))
-            table_words.append(words)
+        load_wu(0)
+        load_words(0)
+        load_wu(1)
+        load_words(1)
         first, second, third = GROUPS
         wd_rows = wd.rearrange("(p j) n -> p j n", j=PACK)
         wd_first = sb("wd_first", [P, PACK, P], F32)
@@ -75,12 +80,14 @@ def tile_list_modp_relu_resb_kernel(
             nc.sync.dma_start(gate[:, lo:hi], wgo[:, lo:hi])
 
         load_gate(*first)
-        wd_rest = sb("wd_rest", [P, PACK, N - P], F32)
-        nc.sync.dma_start(wd_rest[:], wd_rows[:, :, P:])
+        wd_second = sb("wd_second", [P, PACK, P], F32)
+        nc.sync.dma_start(wd_second[:], wd_rows[:, :, P : 2 * P])
+        wd_rest = sb("wd_rest", [P, PACK, N - 2 * P], F32)
+        nc.sync.dma_start(wd_rest[:], wd_rows[:, :, 2 * P :])
         load_gate(*second)
-        nc.sync.dma_start(residual[1][:], rT[P : 2 * P, :])
-        load_gate(*third)
-        for c in range(2, BLOCKS):
+        for c in range(1, BLOCKS):
+            if c == BLOCKS - 1:
+                load_gate(*third)
             nc.sync.dma_start(residual[c][:], rT[c * P : (c + 1) * P, :])
 
         pages = [sb("page%d" % i, [P, T], F32) for i in range(2)]
@@ -88,10 +95,7 @@ def tile_list_modp_relu_resb_kernel(
         nc.gpsimd.memset(pages[1][:], 0.0)
 
         v_scales = sb("v_scales", [P, J], U8)
-        nc.vector.tensor_copy(v_scales[:], table_scales[:].indirect(offsets[:]))
-
         bias_cols = sb("bias_cols", [P, BLOCKS * 32], F32)
-        nc.vector.transpose(bias_cols[:], bias_rows[:])
 
         def scalar_round(dst, src):
             nc.scalar.activation(dst, src, ACT.Copy)
@@ -100,9 +104,9 @@ def tile_list_modp_relu_resb_kernel(
         wu_scales = [sb("wu_scales%d" % a, [P, R], U8) for a in range(PASSES)]
         v_words = [sb("v_words%d" % a, [P, J], U32) for a in range(PASSES)]
 
-        def quantize_wu(a):
+        def quantize_wu(a, copies):
             rounded = [sb("wu_bf%d_%d" % (a, half), [P, 2 * R], BF16) for half in range(2)]
-            for half, copy in enumerate((nc.vector.tensor_copy, scalar_round)):
+            for half, copy in enumerate(copies):
                 copy(
                     rounded[half][:].rearrange("p (t m j) -> p m j t", t=2, j=PACK),
                     wu_raw[a][:].rearrange("p j (m t) -> p m j t", t=PACK)[:, :, :, 2 * half : 2 * half + 2],
@@ -125,18 +129,20 @@ def tile_list_modp_relu_resb_kernel(
                     stop=(a == PASSES - 1 and t == PACK - 1),
                 )
 
-        quantize_wu(0)
+        nc.vector.transpose(bias_cols[:], bias_rows[:])
+        nc.vector.tensor_copy(v_scales[:], table_scales[:].indirect(offsets[:]))
+        quantize_wu(0, (nc.vector.tensor_copy, scalar_round))
         for lo, hi in GROUPS:
             nc.vector.tensor_copy(v_words[0][:, lo:hi], table_words[0][:].indirect(listed(lo, hi)))
         banks = [psum.tile([P, PACK, CHUNK], F32, name="bank%d" % chunk) for chunk in range(CHUNKS)]
         for chunk in range(CHUNKS):
             up_pass(banks[chunk], 0, chunk)
-        quantize_wu(1)
+        quantize_wu(1, (nc.vector.tensor_copy, scalar_round))
         for lo in range(0, J, 256):
             nc.vector.tensor_copy(v_words[1][:, lo : lo + 256], table_words[1][:].indirect(listed(lo, lo + 256)))
 
-        def round_wd(name, raw, width):
-            rounded = sb(name, [P, PACK * width], BF16)
+        def round_wd(name, raw, width, on=None):
+            rounded = sb(name, [P, PACK * width], BF16, on=on)
             scalar_round(
                 rounded[:].rearrange("p (c i j) -> p c j i", i=4, j=PACK),
                 raw[:].rearrange("p j (c i) -> p c j i", i=4),
@@ -160,11 +166,12 @@ def tile_list_modp_relu_resb_kernel(
 
         def finish_up(lo, hi):
             for chunk in range(lo // CHUNK, hi // CHUNK):
-                up_pass(banks[chunk], 1, chunk)
+                bank = banks[chunk]
+                up_pass(bank, 1, chunk)
                 at = PACK * (CHUNK * chunk - lo)
                 nc.scalar.activation(
                     h_bf[lo][:, at : at + PACK * CHUNK].rearrange("p (n t) -> p n t", t=PACK),
-                    banks[chunk][:].rearrange("p t n -> p n t"),
+                    bank[:].rearrange("p t n -> p n t"),
                     ACT.Relu,
                 )
 
@@ -175,8 +182,8 @@ def tile_list_modp_relu_resb_kernel(
 
         down_count = []
 
-        def down(c, groups):
-            bank = psum.tile([P, 512], F32, name="bank%d" % (len(down_count) % BANKS))
+        def down(c, groups, on=None):
+            bank = psum.tile([P, 512], F32, name=on or "bank%d" % (len(down_count) % BANKS))
             down_count.append(c)
             at = 0
             for lo, hi in groups:
@@ -215,8 +222,8 @@ def tile_list_modp_relu_resb_kernel(
             return picked
 
         def sum_from_bank(lo, hi, picked, on=None):
-            total = sb("total0_%d" % lo, [P, hi - lo], F32, on=on)
-            nc.vector.scalar_tensor_tensor(total[:], down(0, [(lo, hi)]), bias_of(0), picked[:], ALU.add, ALU.add)
+            total = sb("total0_%d" % lo, [P, hi - lo], F32)
+            nc.vector.scalar_tensor_tensor(total[:], down(0, [(lo, hi)], on), bias_of(0), picked[:], ALU.add, ALU.add)
             return total
 
         finish_up(*first)
@@ -226,16 +233,15 @@ def tile_list_modp_relu_resb_kernel(
         finish_up(*second)
         quantize_h(*second)
         place(0, *first, total_first)
-        total_second = sum_from_bank(*second, picked_second)
         finish_up(*third)
         quantize_h(*third)
+        total_second = sum_from_bank(*second, picked_second, on="bank%d" % (CHUNKS - 1))
+        quantize_wd(1, 2, round_wd("wd_second_bf", wd_second, P, on="wu_codes0")[:])
         place(0, *second, total_second)
-        wd_rest_bf = round_wd("wd_rest_bf", wd_rest, N - P)
-        quantize_wd(1, 2, wd_rest_bf[:, : PACK * P])
-        quantize_wd(2, BLOCKS, wd_rest_bf[:, PACK * P :])
         y_third = sb("y_third", [P, third[1] - third[0]], F32)
         add_bias(y_third[:], 0, [third])
         waiting = (third, add_residual(0, *third, y_third))
+        quantize_wd(2, BLOCKS, round_wd("wd_rest_bf", wd_rest, N - 2 * P, on="wu_codes1")[:])
         for c in range(1, BLOCKS):
             y = sb("y%d" % c, [P, J], F32)
             add_bias(y[:, : J // 2], c, [first, second])

@@ -45,26 +45,28 @@ def tile_list_modp_relu_resb_kernel(
 
         bias_rows = sb("bias_rows", [P, BLOCKS * 32], F32)
         nc.gpsimd.memset(bias_rows[:], 0.0)
-        nc.sync.dma_start(
-            bias_rows[0:P:32, :].rearrange("q (c i) -> q c i", i=32), b.rearrange("(c q i) -> q c i", q=4, i=32)
-        )
         table_scales = sb("table_scales", [P, T], U8)
         nc.gpsimd.memset(table_scales[:].bitcast(I32), 0)
         wu_raw = [sb("wu_raw%d" % a, [P, PACK, R], F32) for a in range(PASSES)]
         table_words = [sb("table_words%d" % a, [P, T], U32) for a in range(PASSES)]
 
-        def load_wu(a):
-            nc.sync.dma_start(wu_raw[a][:], wu[a * K_PASS : (a + 1) * K_PASS, :].rearrange("(p j) r -> p j r", j=PACK))
+        def load_wu(a, j0=0, j1=PACK):
+            rows = wu[a * K_PASS : (a + 1) * K_PASS, :].rearrange("(p j) r -> p j r", j=PACK)
+            nc.sync.dma_start(wu_raw[a][:, j0:j1], rows[:, j0:j1])
 
         def load_words(a):
             nc.sync.dma_start(table_words[a][:].bitcast(I32), tab_words[a].rearrange("p t i -> p (t i)").bitcast(I32))
 
-        for q in range(4):
+        load_wu(0, 0, 2)
+        nc.sync.dma_start(
+            bias_rows[0:P:32, :].rearrange("q (c i) -> q c i", i=32), b.rearrange("(c q i) -> q c i", q=4, i=32)
+        )
+        for q in (0, 2, 1, 3):
             nc.sync.dma_start(
                 table_scales[32 * q : 32 * q + 4 * PASSES, :].bitcast(I32),
                 tab_scales[:, 4 * q : 4 * q + 4, :].bitcast(I32),
             )
-        load_wu(0)
+        load_wu(0, 2, 4)
         load_words(0)
         load_wu(1)
         load_words(1)
@@ -86,14 +88,18 @@ def tile_list_modp_relu_resb_kernel(
         nc.sync.dma_start(wd_rest[:], wd_rows[:, :, 2 * P :])
         load_gate(*second)
         for c in range(1, BLOCKS):
-            if c == BLOCKS - 1:
+            if c == 2:
                 load_gate(*third)
             nc.sync.dma_start(residual[c][:], rT[c * P : (c + 1) * P, :])
 
         pages = [sb("page%d" % i, [P, T], F32) for i in range(2)]
-        nc.vector.memset(pages[0][:], 0.0)
         nc.gpsimd.memset(pages[1][:], 0.0)
 
+        warm = sb("warm", [P, 2], F32)
+        nc.vector.memset(warm[:, 0:1], 0.0)
+        nc.scalar.activation(warm[:, 1:2], warm[:, 0:1], ACT.Copy)
+
+        nc.vector.memset(pages[0][:], 0.0)
         v_scales = sb("v_scales", [P, J], U8)
         bias_cols = sb("bias_cols", [P, BLOCKS * 32], F32)
 
@@ -202,11 +208,11 @@ def tile_list_modp_relu_resb_kernel(
         def bias_of(c):
             return bias_cols[:, 32 * c : 32 * c + 1]
 
-        def add_bias(dst, c, groups):
-            nc.scalar.activation(dst, down(c, groups), ACT.Identity, bias=bias_of(c))
+        def add_bias(dst, c, groups, on=None):
+            nc.scalar.activation(dst, down(c, groups, on), ACT.Identity, bias=bias_of(c))
 
-        def add_residual(c, lo, hi, y):
-            total = sb("total%d_%d" % (c, lo), [P, hi - lo], F32)
+        def add_residual(c, lo, hi, y, on=None):
+            total = sb("total%d_%d" % (c, lo), [P, hi - lo], F32, on=on)
             nc.vector.tensor_tensor(total[:], residual[c][:].indirect(listed(lo, hi)), y[:], ALU.add)
             return total
 
@@ -239,16 +245,21 @@ def tile_list_modp_relu_resb_kernel(
         quantize_wd(1, 2, round_wd("wd_second_bf", wd_second, P, on="wu_codes0")[:])
         place(0, *second, total_second)
         y_third = sb("y_third", [P, third[1] - third[0]], F32)
-        add_bias(y_third[:], 0, [third])
+        add_bias(y_third[:], 0, [third], "bank2")
         waiting = (third, add_residual(0, *third, y_third))
-        quantize_wd(2, BLOCKS, round_wd("wd_rest_bf", wd_rest, N - 2 * P, on="wu_codes1")[:])
+        ys = {c: sb("y%d" % c, [P, J], F32) for c in range(1, BLOCKS)}
+        add_bias(ys[1][:, : J // 2], 1, [first, second], "bank3")
+        add_bias(ys[1][:, J // 2 :], 1, [third], "bank2")
+        quantize_wd(2, BLOCKS, round_wd("wd_rest_bf", wd_rest, N - 2 * P, on="wu_codes1")[:], on="wd_codes1")
+        place(0, *waiting[0], waiting[1])
+        store(0)
+        add_bias(ys[2][:, : J // 2], 2, [first, second], "bank4")
+        add_bias(ys[2][:, J // 2 :], 2, [third], "bank5")
+        add_bias(ys[3][:, : J // 2], 3, [first, second], "bank4")
+        add_bias(ys[3][:, J // 2 :], 3, [third], "bank5")
+        total = add_residual(1, 0, J, ys[1], on="wd_codes1")
         for c in range(1, BLOCKS):
-            y = sb("y%d" % c, [P, J], F32)
-            add_bias(y[:, : J // 2], c, [first, second])
-            add_bias(y[:, J // 2 :], c, [third])
-            total = add_residual(c, 0, J, y)
-            place(c - 1, *waiting[0], waiting[1])
-            store(c - 1)
-            waiting = ((0, J), total)
-        place(BLOCKS - 1, *waiting[0], waiting[1])
-        store(BLOCKS - 1)
+            ahead = add_residual(c + 1, 0, J, ys[c + 1], on="h_codes512" if c == 1 else None) if c + 1 < BLOCKS else None
+            place(c, 0, J, total)
+            store(c)
+            total = ahead

@@ -234,15 +234,17 @@ def tile_list_modp_relu_resb_kernel(
 
         finish_up(*first)
         quantize_h(*first)
-        picked_first, picked_second = pick(*first), pick(*second)
+        picked_first = pick(*first)
         total_first = sum_from_bank(*first, picked_first)
         finish_up(*second)
         quantize_h(*second)
         place(0, *first, total_first)
+        y_second = sb("y_second", [P, second[1] - second[0]], F32)
+        add_bias(y_second[:], 0, [second], "bank1")
         finish_up(*third)
+        total_second = add_residual(0, *second, y_second, on="wu_codes0")
         quantize_h(*third)
-        total_second = sum_from_bank(*second, picked_second, on="bank%d" % (CHUNKS - 1))
-        quantize_wd(1, 2, round_wd("wd_second_bf", wd_second, P, on="wu_codes0")[:])
+        quantize_wd(1, 2, round_wd("wd_second_bf", wd_second, P, on="wu_scales1")[:])
         place(0, *second, total_second)
         y_third = sb("y_third", [P, third[1] - third[0]], F32)
         add_bias(y_third[:], 0, [third], "bank2")

@@ -23,6 +23,8 @@ BLOCKS = N // P
 CHUNK = 128
 CHUNKS = J // CHUNK
 BANKS = 8
+UP_BANKS = 7
+VECTOR_SHARE = 40
 GROUPS = ((0, 256), (256, 512), (512, 1024))
 
 
@@ -108,7 +110,9 @@ def tile_list_modp_relu_resb_kernel(
 
         wu_codes = [sb("wu_codes%d" % a, [P, R], U32) for a in range(PASSES)]
         wu_scales = [sb("wu_scales%d" % a, [P, R], U8) for a in range(PASSES)]
-        v_words = [sb("v_words%d" % a, [P, J], U32) for a in range(PASSES)]
+        v_words = [
+            [sb("v_words%d_%d" % (a, lo), [P, 256], U32) for lo in range(0, J, 256)] for a in range(PASSES)
+        ]
 
         def quantize_wu(a, copies):
             rounded = [sb("wu_bf%d_%d" % (a, half), [P, 2 * R], BF16) for half in range(2)]
@@ -129,7 +133,7 @@ def tile_list_modp_relu_resb_kernel(
                     bank[:, t, :],
                     lhsT=wu_codes[a][:, w_cols].bitcast(FP8X4),
                     lhsT_scale=wu_scales[a][:, w_cols],
-                    rhs=v_words[a][:, cols].bitcast(FP8X4),
+                    rhs=v_words[a][chunk // 2][:, (chunk % 2) * CHUNK : (chunk % 2 + 1) * CHUNK].bitcast(FP8X4),
                     rhs_scale=v_scales[4 * a :, cols],
                     start=(a == 0 and t == 0),
                     stop=(a == PASSES - 1 and t == PACK - 1),
@@ -137,19 +141,24 @@ def tile_list_modp_relu_resb_kernel(
 
         nc.vector.transpose(bias_cols[:], bias_rows[:])
         nc.vector.tensor_copy(v_scales[:], table_scales[:].indirect(offsets[:]))
-        quantize_wu(0, (nc.vector.tensor_copy, scalar_round))
-        for lo, hi in GROUPS:
-            nc.vector.tensor_copy(v_words[0][:, lo:hi], table_words[0][:].indirect(listed(lo, hi)))
-        banks = [psum.tile([P, PACK, CHUNK], F32, name="bank%d" % chunk) for chunk in range(CHUNKS)]
-        for chunk in range(CHUNKS):
+        rounded = sb("wu_bf0", [P, PACK * R], BF16)
+        slots_out = rounded[:].rearrange("p (t m j) -> p m j t", t=PACK, j=PACK)
+        slots_in = wu_raw[0][:].rearrange("p j (m t) -> p m j t", t=PACK)
+        nc.vector.tensor_copy(slots_out[:, :VECTOR_SHARE], slots_in[:, :VECTOR_SHARE])
+        scalar_round(slots_out[:, VECTOR_SHARE:], slots_in[:, VECTOR_SHARE:])
+        nc.vector.quantize_mx(wu_codes[0][:].bitcast(FP8X4), wu_scales[0][:], rounded[:])
+        for lo in range(0, J, 256):
+            nc.vector.tensor_copy(v_words[0][lo // 256][:], table_words[0][:].indirect(listed(lo, lo + 256)))
+        banks = [psum.tile([P, PACK, CHUNK], F32, name="bank%d" % chunk) for chunk in range(UP_BANKS)]
+        for chunk in range(UP_BANKS):
             up_pass(banks[chunk], 0, chunk)
         quantize_wu(1, (nc.vector.tensor_copy, scalar_round))
         for lo in range(0, J, 256):
-            nc.vector.tensor_copy(v_words[1][:, lo : lo + 256], table_words[1][:].indirect(listed(lo, lo + 256)))
+            nc.vector.tensor_copy(v_words[1][lo // 256][:], table_words[1][:].indirect(listed(lo, lo + 256)))
 
-        def round_wd(name, raw, width, on=None):
+        def round_wd(name, raw, width, on=None, copy=scalar_round):
             rounded = sb(name, [P, PACK * width], BF16, on=on)
-            scalar_round(
+            copy(
                 rounded[:].rearrange("p (c i j) -> p c j i", i=4, j=PACK),
                 raw[:].rearrange("p j (c i) -> p c j i", i=4),
             )
@@ -165,15 +174,16 @@ def tile_list_modp_relu_resb_kernel(
                 wd_codes[c] = codes[:, (c - c0) * P : (c - c0 + 1) * P]
                 wd_scales[c] = scales[:, (c - c0) * P : (c - c0 + 1) * P]
 
-        quantize_wd(0, 1, round_wd("wd_first_bf", wd_first, P)[:])
+        wd_first_bf = round_wd("wd_first_bf", wd_first, P, copy=nc.vector.tensor_copy)
 
-        h_bf = {lo: sb("h_bf%d" % lo, [P, PACK * (hi - lo)], BF16, on=None if lo else "wd_first") for lo, hi in GROUPS}
+        h_bf = {lo: sb("h_bf%d" % lo, [P, PACK * (hi - lo)], BF16) for lo, hi in GROUPS}
         h_codes, h_scales = {}, {}
 
         def finish_up(lo, hi):
             for chunk in range(lo // CHUNK, hi // CHUNK):
                 bank = banks[chunk]
-                up_pass(bank, 1, chunk)
+                if chunk < 4:
+                    up_pass(bank, 1, chunk)
                 at = PACK * (CHUNK * chunk - lo)
                 nc.scalar.activation(
                     h_bf[lo][:, at : at + PACK * CHUNK].rearrange("p (n t) -> p n t", t=PACK),
@@ -233,11 +243,18 @@ def tile_list_modp_relu_resb_kernel(
             return total
 
         finish_up(*first)
-        quantize_h(*first)
-        picked_first = pick(*first)
-        total_first = sum_from_bank(*first, picked_first)
         finish_up(*second)
-        quantize_h(*second)
+        up_pass(banks[4], 1, 4)
+        up_pass(banks[5], 1, 5)
+        quantize_h(*first)
+        quantize_wd(0, 1, wd_first_bf[:], on="v_words1_512")
+        picked_first = pick(*first)
+        up_pass(banks[6], 1, 6)
+        banks.append(psum.tile([P, PACK, CHUNK], F32, name="bank0"))
+        up_pass(banks[7], 0, 7)
+        up_pass(banks[7], 1, 7)
+        quantize_h(*second, on="v_words1_768")
+        total_first = sum_from_bank(*first, picked_first, "bank7")
         place(0, *first, total_first)
         y_second = sb("y_second", [P, second[1] - second[0]], F32)
         add_bias(y_second[:], 0, [second], "bank1")

@@ -23,7 +23,8 @@ BLOCKS = N // P
 CHUNK = 128
 CHUNKS = J // CHUNK
 BANKS = 8
-UP_BANKS = 7
+WU_AHEAD = 896
+UP_BANKS = 6
 VECTOR_SHARE = 40
 GROUPS = ((0, 256), (256, 512), (512, 1024))
 
@@ -46,29 +47,29 @@ def tile_list_modp_relu_resb_kernel(
             return offsets[:, lo // 16 : hi // 16]
 
         bias_rows = sb("bias_rows", [P, BLOCKS * 32], F32)
-        nc.gpsimd.memset(bias_rows[:], 0.0)
         table_scales = sb("table_scales", [P, T], U8)
         nc.gpsimd.memset(table_scales[:].bitcast(I32), 0)
+        nc.gpsimd.memset(bias_rows[:], 0.0)
         wu_raw = [sb("wu_raw%d" % a, [P, PACK, R], F32) for a in range(PASSES)]
         table_words = [sb("table_words%d" % a, [P, T], U32) for a in range(PASSES)]
 
-        def load_wu(a, j0=0, j1=PACK):
-            rows = wu[a * K_PASS : (a + 1) * K_PASS, :].rearrange("(p j) r -> p j r", j=PACK)
-            nc.sync.dma_start(wu_raw[a][:, j0:j1], rows[:, j0:j1])
+        def load_wu(a, lo=0, hi=PACK * R):
+            rows = wu[a * K_PASS : (a + 1) * K_PASS, :].rearrange("(p j) r -> p (j r)", j=PACK)
+            nc.sync.dma_start(wu_raw[a][:].rearrange("p j r -> p (j r)")[:, lo:hi], rows[:, lo:hi])
 
         def load_words(a):
             nc.sync.dma_start(table_words[a][:].bitcast(I32), tab_words[a].rearrange("p t i -> p (t i)").bitcast(I32))
 
-        load_wu(0, 0, 2)
-        nc.sync.dma_start(
-            bias_rows[0:P:32, :].rearrange("q (c i) -> q c i", i=32), b.rearrange("(c q i) -> q c i", q=4, i=32)
-        )
+        load_wu(0, 0, WU_AHEAD)
         for q in (0, 2, 1, 3):
             nc.sync.dma_start(
                 table_scales[32 * q : 32 * q + 4 * PASSES, :].bitcast(I32),
                 tab_scales[:, 4 * q : 4 * q + 4, :].bitcast(I32),
             )
-        load_wu(0, 2, 4)
+        nc.sync.dma_start(
+            bias_rows[0:P:32, :].rearrange("q (c i) -> q c i", i=32), b.rearrange("(c q i) -> q c i", q=4, i=32)
+        )
+        load_wu(0, WU_AHEAD, PACK * R)
         load_words(0)
         load_wu(1)
         load_words(1)
@@ -249,17 +250,16 @@ def tile_list_modp_relu_resb_kernel(
         quantize_h(*first)
         quantize_wd(0, 1, wd_first_bf[:], on="v_words1_512")
         picked_first = pick(*first)
-        up_pass(banks[6], 1, 6)
-        banks.append(psum.tile([P, PACK, CHUNK], F32, name="bank0"))
-        up_pass(banks[7], 0, 7)
-        up_pass(banks[7], 1, 7)
-        quantize_h(*second, on="v_words1_768")
+        picked_second = pick(*second)
         total_first = sum_from_bank(*first, picked_first, "bank7")
+        for chunk in (6, 7):
+            banks.append(psum.tile([P, PACK, CHUNK], F32, name="bank%d" % (chunk % UP_BANKS)))
+            up_pass(banks[chunk], 0, chunk)
+            up_pass(banks[chunk], 1, chunk)
+        quantize_h(*second, on="v_words1_768")
         place(0, *first, total_first)
-        y_second = sb("y_second", [P, second[1] - second[0]], F32)
-        add_bias(y_second[:], 0, [second], "bank1")
+        total_second = sum_from_bank(*second, picked_second, "bank6")
         finish_up(*third)
-        total_second = add_residual(0, *second, y_second, on="wu_codes0")
         quantize_h(*third)
         quantize_wd(1, 2, round_wd("wd_second_bf", wd_second, P, on="wu_scales1")[:])
         place(0, *second, total_second)

@@ -23,9 +23,9 @@ BLOCKS = N // P
 CHUNK = 128
 CHUNKS = J // CHUNK
 BANKS = 8
-WU_AHEAD = 896
+WU_AHEAD = 768
 UP_BANKS = 6
-VECTOR_SHARE = 40
+VECTOR_SHARE = 48
 GROUPS = ((0, 256), (256, 512), (512, 1024))
 
 
@@ -66,12 +66,12 @@ def tile_list_modp_relu_resb_kernel(
                 table_scales[32 * q : 32 * q + 4 * PASSES, :].bitcast(I32),
                 tab_scales[:, 4 * q : 4 * q + 4, :].bitcast(I32),
             )
-        nc.sync.dma_start(
-            bias_rows[0:P:32, :].rearrange("q (c i) -> q c i", i=32), b.rearrange("(c q i) -> q c i", q=4, i=32)
-        )
         load_wu(0, WU_AHEAD, PACK * R)
         load_words(0)
         load_wu(1)
+        nc.sync.dma_start(
+            bias_rows[0:P:32, :].rearrange("q (c i) -> q c i", i=32), b.rearrange("(c q i) -> q c i", q=4, i=32)
+        )
         load_words(1)
         first, second, third = GROUPS
         wd_rows = wd.rearrange("(p j) n -> p j n", j=PACK)
@@ -122,6 +122,7 @@ def tile_list_modp_relu_resb_kernel(
                     rounded[half][:].rearrange("p (t m j) -> p m j t", t=2, j=PACK),
                     wu_raw[a][:].rearrange("p j (m t) -> p m j t", t=PACK)[:, :, :, 2 * half : 2 * half + 2],
                 )
+            nc.vector.transpose(bias_cols[:], bias_rows[:])
             for half in range(2):
                 cols = slice(2 * P * half, 2 * P * (half + 1))
                 nc.vector.quantize_mx(wu_codes[a][:, cols].bitcast(FP8X4), wu_scales[a][:, cols], rounded[half][:])
@@ -140,7 +141,6 @@ def tile_list_modp_relu_resb_kernel(
                     stop=(a == PASSES - 1 and t == PACK - 1),
                 )
 
-        nc.vector.transpose(bias_cols[:], bias_rows[:])
         nc.vector.tensor_copy(v_scales[:], table_scales[:].indirect(offsets[:]))
         rounded = sb("wu_bf0", [P, PACK * R], BF16)
         slots_out = rounded[:].rearrange("p (t m j) -> p m j t", t=PACK, j=PACK)

@@ -175,7 +175,10 @@ def tile_list_modp_relu_resb_kernel(
                 wd_codes[c] = codes[:, (c - c0) * P : (c - c0 + 1) * P]
                 wd_scales[c] = scales[:, (c - c0) * P : (c - c0 + 1) * P]
 
-        wd_first_bf = round_wd("wd_first_bf", wd_first, P, copy=nc.vector.tensor_copy)
+        wd_first_bf = sb("wd_first_bf", [P, PACK * P], BF16)
+        nc.gpsimd.tensor_copy(
+            wd_first_bf[:].rearrange("p (n j) -> p n j", j=PACK), wd_first[:].rearrange("p j n -> p n j")
+        )
 
         h_bf = {lo: sb("h_bf%d" % lo, [P, PACK * (hi - lo)], BF16) for lo, hi in GROUPS}
         h_codes, h_scales = {}, {}
@@ -247,8 +250,8 @@ def tile_list_modp_relu_resb_kernel(
         finish_up(*second)
         up_pass(banks[4], 1, 4)
         up_pass(banks[5], 1, 5)
+        quantize_wd(0, 1, wd_first_bf[:])
         quantize_h(*first)
-        quantize_wd(0, 1, wd_first_bf[:], on="v_words1_512")
         picked_first = pick(*first)
         picked_second = pick(*second)
         total_first = sum_from_bank(*first, picked_first, "bank7")

@@ -1,6 +1,7 @@
 from contextlib import ExitStack
 
 import concourse.mybir as mybir
+from concourse.masks import make_identity
 
 K, R, N, T, J = 1024, 512, 512, 2048, 1024
 FLOPS = 2 * K * R * J + 2 * R * N * J
@@ -26,6 +27,7 @@ BANKS = 8
 WU_AHEAD = 768
 UP_BANKS = 6
 VECTOR_SHARE = 48
+HEAD = 64
 GROUPS = ((0, 256), (256, 512), (512, 1024))
 
 
@@ -35,6 +37,7 @@ def tile_list_modp_relu_resb_kernel(
     nc = tc.nc
     with ExitStack() as ctx:
         keep = ctx.enter_context(tc.tile_pool(name="keep", bufs=1))
+        shared = ctx.enter_context(tc.tile_pool(name="shared", bufs=1))
         psum = ctx.enter_context(tc.psum_pool(name="psum", bufs=1))
 
         def sb(name, shape, dtype, on=None):
@@ -46,10 +49,12 @@ def tile_list_modp_relu_resb_kernel(
         def listed(lo, hi):
             return offsets[:, lo // 16 : hi // 16]
 
-        bias_rows = sb("bias_rows", [P, BLOCKS * 32], F32)
+        bias_rows = sb("bias_rows", [P, P], F32)
         table_scales = sb("table_scales", [P, T], U8)
         nc.gpsimd.memset(table_scales[:].bitcast(I32), 0)
         nc.gpsimd.memset(bias_rows[:], 0.0)
+        identity = sb("identity", [P, P], F32)
+        make_identity(nc, identity[:])
         wu_raw = [sb("wu_raw%d" % a, [P, PACK, R], F32) for a in range(PASSES)]
         table_words = [sb("table_words%d" % a, [P, T], U32) for a in range(PASSES)]
 
@@ -72,6 +77,10 @@ def tile_list_modp_relu_resb_kernel(
         nc.sync.dma_start(
             bias_rows[0:P:32, :].rearrange("q (c i) -> q c i", i=32), b.rearrange("(c q i) -> q c i", q=4, i=32)
         )
+        nc.sync.dma_start(
+            bias_rows[1:P:32, :64].rearrange("q (c i) -> q c i", i=32),
+            wgo[0, :256].rearrange("(c q i) -> q c i", q=4, i=32),
+        )
         load_words(1)
         first, second, third = GROUPS
         wd_rows = wd.rearrange("(p j) n -> p j n", j=PACK)
@@ -84,7 +93,6 @@ def tile_list_modp_relu_resb_kernel(
         def load_gate(lo, hi):
             nc.sync.dma_start(gate[:, lo:hi], wgo[:, lo:hi])
 
-        load_gate(*first)
         wd_second = sb("wd_second", [P, PACK, P], F32)
         nc.sync.dma_start(wd_second[:], wd_rows[:, :, P : 2 * P])
         wd_rest = sb("wd_rest", [P, PACK, N - 2 * P], F32)
@@ -111,9 +119,18 @@ def tile_list_modp_relu_resb_kernel(
 
         wu_codes = [sb("wu_codes%d" % a, [P, R], U32) for a in range(PASSES)]
         wu_scales = [sb("wu_scales%d" % a, [P, R], U8) for a in range(PASSES)]
-        v_words = [
-            [sb("v_words%d_%d" % (a, lo), [P, 256], U32) for lo in range(0, J, 256)] for a in range(PASSES)
-        ]
+        cuts = (((0, 256), (256, 512), (512, 768), (768, J)),) * 2
+        v_words = [[sb("v_words%d_%d" % (a, lo), [P, hi - lo], U32) for lo, hi in cuts[a]] for a in range(PASSES)]
+
+        def gather_words(a):
+            for (lo, hi), words in zip(cuts[a], v_words[a]):
+                nc.vector.tensor_copy(words[:], table_words[a][:].indirect(listed(lo, hi)))
+
+        def words_of(a, chunk):
+            at = chunk * CHUNK
+            return [
+                words[:, at - lo : at - lo + CHUNK] for (lo, hi), words in zip(cuts[a], v_words[a]) if lo <= at < hi
+            ][0]
 
         def quantize_wu(a, copies):
             rounded = [sb("wu_bf%d_%d" % (a, half), [P, 2 * R], BF16) for half in range(2)]
@@ -135,7 +152,7 @@ def tile_list_modp_relu_resb_kernel(
                     bank[:, t, :],
                     lhsT=wu_codes[a][:, w_cols].bitcast(FP8X4),
                     lhsT_scale=wu_scales[a][:, w_cols],
-                    rhs=v_words[a][chunk // 2][:, (chunk % 2) * CHUNK : (chunk % 2 + 1) * CHUNK].bitcast(FP8X4),
+                    rhs=words_of(a, chunk).bitcast(FP8X4),
                     rhs_scale=v_scales[4 * a :, cols],
                     start=(a == 0 and t == 0),
                     stop=(a == PASSES - 1 and t == PACK - 1),
@@ -148,14 +165,20 @@ def tile_list_modp_relu_resb_kernel(
         nc.vector.tensor_copy(slots_out[:, :VECTOR_SHARE], slots_in[:, :VECTOR_SHARE])
         scalar_round(slots_out[:, VECTOR_SHARE:], slots_in[:, VECTOR_SHARE:])
         nc.vector.quantize_mx(wu_codes[0][:].bitcast(FP8X4), wu_scales[0][:], rounded[:])
-        for lo in range(0, J, 256):
-            nc.vector.tensor_copy(v_words[0][lo // 256][:], table_words[0][:].indirect(listed(lo, lo + 256)))
+        gather_words(0)
         banks = [psum.tile([P, PACK, CHUNK], F32, name="bank%d" % chunk) for chunk in range(UP_BANKS)]
         for chunk in range(UP_BANKS):
             up_pass(banks[chunk], 0, chunk)
         quantize_wu(1, (nc.vector.tensor_copy, scalar_round))
-        for lo in range(0, J, 256):
-            nc.vector.tensor_copy(v_words[1][lo // 256][:], table_words[1][:].indirect(listed(lo, lo + 256)))
+        spread = psum.tile([P, 2, P], F32, name="bank6")
+        for c in range(2):
+            at = 32 * c + 1
+            nc.tensor.transpose(spread[:, c, :], bias_cols[:, at : at + 1].to_broadcast([P, P]), identity[:])
+        gate_head = shared.tile([P, HEAD], F32, name="gate_head", offset=1024 - 2 * HEAD, align_bytes=64)
+        nc.scalar.activation(gate_head[:], spread[:, 0, :HEAD], ACT.Copy)
+        nc.scalar.activation(gate[:, : 2 * P], spread[:].rearrange("p c j -> p (c j)"), ACT.Copy)
+        gate_first = {(0, HEAD): gate_head[:], (HEAD, 2 * P): gate[:, HEAD : 2 * P]}
+        gather_words(1)
 
         def round_wd(name, raw, width, on=None, copy=scalar_round):
             rounded = sb(name, [P, PACK * width], BF16, on=on)
@@ -195,9 +218,9 @@ def tile_list_modp_relu_resb_kernel(
                     ACT.Relu,
                 )
 
-        def quantize_h(lo, hi, on=None):
+        def quantize_h(lo, hi, on=None, scales=None):
             h_codes[lo] = sb("h_codes%d" % lo, [P, hi - lo], U32, on=on)
-            h_scales[lo] = sb("h_scales%d" % lo, [P, hi - lo], U8)
+            h_scales[lo] = scales if scales is not None else sb("h_scales%d" % lo, [P, hi - lo], U8)
             nc.vector.quantize_mx(h_codes[lo][:].bitcast(FP8X4), h_scales[lo][:], h_bf[lo][:])
 
         down_count = []
@@ -236,42 +259,39 @@ def tile_list_modp_relu_resb_kernel(
         def store(c):
             nc.sync.dma_start(out[c * P : (c + 1) * P, :], pages[c % 2][:])
 
-        def pick(lo, hi):
-            picked = sb("picked%d" % lo, [P, hi - lo], F32)
-            nc.vector.tensor_copy(picked[:], residual[0][:].indirect(listed(lo, hi)))
-            return picked
-
-        def sum_from_bank(lo, hi, picked, on=None):
-            total = sb("total0_%d" % lo, [P, hi - lo], F32)
-            nc.vector.scalar_tensor_tensor(total[:], down(0, [(lo, hi)], on), bias_of(0), picked[:], ALU.add, ALU.add)
-            return total
-
         finish_up(*first)
         finish_up(*second)
         up_pass(banks[4], 1, 4)
         up_pass(banks[5], 1, 5)
         quantize_wd(0, 1, wd_first_bf[:])
         quantize_h(*first)
-        picked_first = pick(*first)
-        picked_second = pick(*second)
-        total_first = sum_from_bank(*first, picked_first, "bank7")
+        gated_residual = sb("gated_residual", [P, 256], F32)
+        for (lo, hi), factor in gate_first.items():
+            nc.vector.tensor_tensor(gated_residual[:, lo:hi], residual[0][:].indirect(listed(lo, hi)), factor, ALU.mult)
+        gated_y = shared.tile([P, 256], F32, name="gated_y", offset=0, align_bytes=64)
+        nc.vector.scalar_tensor_tensor(
+            gated_y[:], down(0, [first], "bank7"), bias_of(0), gate[:, first[0] : first[1]], ALU.add, ALU.mult
+        )
         for chunk in (6, 7):
-            banks.append(psum.tile([P, PACK, CHUNK], F32, name="bank%d" % (chunk % UP_BANKS)))
+            banks.append(psum.tile([P, PACK, CHUNK], F32, name="bank%d" % (chunk - 4)))
             up_pass(banks[chunk], 0, chunk)
             up_pass(banks[chunk], 1, chunk)
-        quantize_h(*second, on="v_words1_768")
-        place(0, *first, total_first)
-        total_second = sum_from_bank(*second, picked_second, "bank6")
+        second_scales = shared.tile([P, 256], U8, name="second_scales", offset=1024, align_bytes=64)
+        quantize_h(*second, scales=second_scales)
+        nc.vector.tensor_tensor(pages[0][:].indirect(listed(*first)), gated_residual[:], gated_y[:], ALU.add)
+        y_second = sb("y_second", [P, second[1] - second[0]], F32)
+        add_bias(y_second[:], 0, [second], "bank6")
+        total_second = add_residual(0, *second, y_second)
         finish_up(*third)
         quantize_h(*third)
         quantize_wd(1, 2, round_wd("wd_second_bf", wd_second, P, on="wu_scales1")[:])
         place(0, *second, total_second)
         y_third = sb("y_third", [P, third[1] - third[0]], F32)
-        add_bias(y_third[:], 0, [third], "bank2")
+        add_bias(y_third[:], 0, [third], "bank0")
         waiting = (third, add_residual(0, *third, y_third))
         ys = {c: sb("y%d" % c, [P, J], F32) for c in range(1, BLOCKS)}
-        add_bias(ys[1][:, : J // 2], 1, [first, second], "bank3")
-        add_bias(ys[1][:, J // 2 :], 1, [third], "bank2")
+        add_bias(ys[1][:, : J // 2], 1, [first, second], "bank1")
+        add_bias(ys[1][:, J // 2 :], 1, [third], "bank0")
         quantize_wd(2, BLOCKS, round_wd("wd_rest_bf", wd_rest, N - 2 * P, on="wu_codes1")[:], on="wd_codes1")
         place(0, *waiting[0], waiting[1])
         store(0)

@@ -119,7 +119,7 @@ def tile_list_modp_relu_resb_kernel(
 
         wu_codes = [sb("wu_codes%d" % a, [P, R], U32) for a in range(PASSES)]
         wu_scales = [sb("wu_scales%d" % a, [P, R], U8) for a in range(PASSES)]
-        cuts = (((0, 256), (256, 512), (512, 768), (768, J)),) * 2
+        cuts = (((0, 256), (256, 512), (512, 768), (768, J)), ((0, 128), (128, 256), (256, 512), (512, 768), (768, J)))
         v_words = [[sb("v_words%d_%d" % (a, lo), [P, hi - lo], U32) for lo, hi in cuts[a]] for a in range(PASSES)]
 
         def gather_words(a):

@@ -119,7 +119,7 @@ def tile_list_modp_relu_resb_kernel(
 
         wu_codes = [sb("wu_codes%d" % a, [P, R], U32) for a in range(PASSES)]
         wu_scales = [sb("wu_scales%d" % a, [P, R], U8) for a in range(PASSES)]
-        cuts = (((0, 256), (256, 512), (512, 768), (768, J)), ((0, 128), (128, 256), (256, 512), (512, 768), (768, J)))
+        cuts = (((0, 128), (128, 512), (512, 768), (768, J)), ((0, 128), (128, 256), (256, 512), (512, 768), (768, J)))
         v_words = [[sb("v_words%d_%d" % (a, lo), [P, hi - lo], U32) for lo, hi in cuts[a]] for a in range(PASSES)]
 
         def gather_words(a):
@@ -200,7 +200,12 @@ def tile_list_modp_relu_resb_kernel(
 
         wd_first_bf = sb("wd_first_bf", [P, PACK * P], BF16)
         nc.gpsimd.tensor_copy(
-            wd_first_bf[:].rearrange("p (n j) -> p n j", j=PACK), wd_first[:].rearrange("p j n -> p n j")
+            wd_first_bf[:].rearrange("p (n j) -> p n j", j=PACK)[:, :64],
+            wd_first[:].rearrange("p j n -> p n j")[:, :64],
+        )
+        scalar_round(
+            wd_first_bf[:, PACK * 64 :].rearrange("p (c i j) -> p c j i", i=4, j=PACK),
+            wd_first[:, :, 64:].rearrange("p j (c i) -> p c j i", i=4),
         )
 
         h_bf = {lo: sb("h_bf%d" % lo, [P, PACK * (hi - lo)], BF16) for lo, hi in GROUPS}

@@ -41,7 +41,7 @@ def tile_list_modp_relu_resb_kernel(
         psum = ctx.enter_context(tc.psum_pool(name="psum", bufs=1))
 
         def sb(name, shape, dtype, on=None):
-            return keep.tile(shape, dtype, name=name, tag=on or name, align_bytes=64)
+            return keep.tile(shape, dtype, name=name, tag=on or name, align_bytes=256)
 
         offsets = keep.tile([P, J // 16], U16, name="offsets")
         nc.sync.dma_start(offsets[:], offs)

@@ -44,7 +44,6 @@ def tile_list_modp_relu_resb_kernel(
             return keep.tile(shape, dtype, name=name, tag=on or name, align_bytes=256)
 
         offsets = keep.tile([P, J // 16], U16, name="offsets")
-        nc.sync.dma_start(offsets[:], offs)
 
         def listed(lo, hi):
             return offsets[:, lo // 16 : hi // 16]
@@ -66,6 +65,7 @@ def tile_list_modp_relu_resb_kernel(
             nc.sync.dma_start(table_words[a][:].bitcast(I32), tab_words[a].rearrange("p t i -> p (t i)").bitcast(I32))
 
         load_wu(0, 0, WU_AHEAD)
+        nc.sync.dma_start(offsets[:], offs)
         for q in (0, 2, 1, 3):
             nc.sync.dma_start(
                 table_scales[32 * q : 32 * q + 4 * PASSES, :].bitcast(I32),

from contextlib import ExitStack

import concourse.mybir as mybir
from concourse.masks import make_identity

K, R, N, T, J = 1024, 512, 512, 2048, 1024
FLOPS = 2 * K * R * J + 2 * R * N * J

F32 = mybir.dt.float32
BF16 = mybir.dt.bfloat16
I32 = mybir.dt.int32
U32 = mybir.dt.uint32
U16 = mybir.dt.uint16
U8 = mybir.dt.uint8
FP8X4 = mybir.dt.float8_e4m3fn_x4
ACT = mybir.ActivationFunctionType
ALU = mybir.AluOpType

P = 128
PACK = 4
K_PASS = P * PACK
PASSES = K // K_PASS
BLOCKS = N // P
CHUNK = 128
CHUNKS = J // CHUNK
BANKS = 8
WU_AHEAD = 768
UP_BANKS = 6
VECTOR_SHARE = 48
HEAD = 64
GROUPS = ((0, 256), (256, 512), (512, 1024))


def tile_list_modp_relu_resb_kernel(
    tc, tab_words, tab_scales, wu, wd, rT, b, wgo, offs, out
):
    nc = tc.nc
    with ExitStack() as ctx:
        keep = ctx.enter_context(tc.tile_pool(name="keep", bufs=1))
        shared = ctx.enter_context(tc.tile_pool(name="shared", bufs=1))
        psum = ctx.enter_context(tc.psum_pool(name="psum", bufs=1))

        def sb(name, shape, dtype, on=None):
            return keep.tile(shape, dtype, name=name, tag=on or name, align_bytes=256)

        offsets = keep.tile([P, J // 16], U16, name="offsets")

        def listed(lo, hi):
            return offsets[:, lo // 16 : hi // 16]

        bias_rows = sb("bias_rows", [P, P], F32)
        table_scales = sb("table_scales", [P, T], U8)
        nc.gpsimd.memset(table_scales[:].bitcast(I32), 0)
        nc.gpsimd.memset(bias_rows[:], 0.0)
        identity = sb("identity", [P, P], F32)
        make_identity(nc, identity[:])
        wu_raw = [sb("wu_raw%d" % a, [P, PACK, R], F32) for a in range(PASSES)]
        table_words = [sb("table_words%d" % a, [P, T], U32) for a in range(PASSES)]

        def load_wu(a, lo=0, hi=PACK * R):
            rows = wu[a * K_PASS : (a + 1) * K_PASS, :].rearrange("(p j) r -> p (j r)", j=PACK)
            nc.sync.dma_start(wu_raw[a][:].rearrange("p j r -> p (j r)")[:, lo:hi], rows[:, lo:hi])

        def load_words(a):
            nc.sync.dma_start(table_words[a][:].bitcast(I32), tab_words[a].rearrange("p t i -> p (t i)").bitcast(I32))

        load_wu(0, 0, WU_AHEAD)
        nc.sync.dma_start(offsets[:], offs)
        for q in (0, 2, 1, 3):
            nc.sync.dma_start(
                table_scales[32 * q : 32 * q + 4 * PASSES, :].bitcast(I32),
                tab_scales[:, 4 * q : 4 * q + 4, :].bitcast(I32),
            )
        load_wu(0, WU_AHEAD, PACK * R)
        load_words(0)
        load_wu(1)
        nc.sync.dma_start(
            bias_rows[0:P:32, :].rearrange("q (c i) -> q c i", i=32), b.rearrange("(c q i) -> q c i", q=4, i=32)
        )
        nc.sync.dma_start(
            bias_rows[1:P:32, :64].rearrange("q (c i) -> q c i", i=32),
            wgo[0, :256].rearrange("(c q i) -> q c i", q=4, i=32),
        )
        load_words(1)
        first, second, third = GROUPS
        wd_rows = wd.rearrange("(p j) n -> p j n", j=PACK)
        wd_first = sb("wd_first", [P, PACK, P], F32)
        nc.sync.dma_start(wd_first[:], wd_rows[:, :, :P])
        residual = [sb("residual%d" % c, [P, T], F32) for c in range(BLOCKS)]
        nc.sync.dma_start(residual[0][:], rT[:P, :])
        gate = sb("gate", [P, J], F32)

        def load_gate(lo, hi):
            nc.sync.dma_start(gate[:, lo:hi], wgo[:, lo:hi])

        wd_second = sb("wd_second", [P, PACK, P], F32)
        nc.sync.dma_start(wd_second[:], wd_rows[:, :, P : 2 * P])
        wd_rest = sb("wd_rest", [P, PACK, N - 2 * P], F32)
        nc.sync.dma_start(wd_rest[:], wd_rows[:, :, 2 * P :])
        load_gate(*second)
        for c in range(1, BLOCKS):
            if c == 2:
                load_gate(*third)
            nc.sync.dma_start(residual[c][:], rT[c * P : (c + 1) * P, :])

        pages = [sb("page%d" % i, [P, T], F32) for i in range(2)]
        nc.gpsimd.memset(pages[1][:], 0.0)

        warm = sb("warm", [P, 2], F32)
        nc.vector.memset(warm[:, 0:1], 0.0)
        nc.scalar.activation(warm[:, 1:2], warm[:, 0:1], ACT.Copy)

        nc.vector.memset(pages[0][:], 0.0)
        v_scales = sb("v_scales", [P, J], U8)
        bias_cols = sb("bias_cols", [P, BLOCKS * 32], F32)

        def scalar_round(dst, src):
            nc.scalar.activation(dst, src, ACT.Copy)

        wu_codes = [sb("wu_codes%d" % a, [P, R], U32) for a in range(PASSES)]
        wu_scales = [sb("wu_scales%d" % a, [P, R], U8) for a in range(PASSES)]
        cuts = (((0, 128), (128, 512), (512, 768), (768, J)), ((0, 128), (128, 256), (256, 512), (512, 768), (768, J)))
        v_words = [[sb("v_words%d_%d" % (a, lo), [P, hi - lo], U32) for lo, hi in cuts[a]] for a in range(PASSES)]

        def gather_words(a):
            for (lo, hi), words in zip(cuts[a], v_words[a]):
                nc.vector.tensor_copy(words[:], table_words[a][:].indirect(listed(lo, hi)))

        def words_of(a, chunk):
            at = chunk * CHUNK
            return [
                words[:, at - lo : at - lo + CHUNK] for (lo, hi), words in zip(cuts[a], v_words[a]) if lo <= at < hi
            ][0]

        def quantize_wu(a, copies):
            rounded = [sb("wu_bf%d_%d" % (a, half), [P, 2 * R], BF16) for half in range(2)]
            for half, copy in enumerate(copies):
                copy(
                    rounded[half][:].rearrange("p (t m j) -> p m j t", t=2, j=PACK),
                    wu_raw[a][:].rearrange("p j (m t) -> p m j t", t=PACK)[:, :, :, 2 * half : 2 * half + 2],
                )
            nc.vector.transpose(bias_cols[:], bias_rows[:])
            for half in range(2):
                cols = slice(2 * P * half, 2 * P * (half + 1))
                nc.vector.quantize_mx(wu_codes[a][:, cols].bitcast(FP8X4), wu_scales[a][:, cols], rounded[half][:])

        def up_pass(bank, a, chunk):
            cols = slice(chunk * CHUNK, (chunk + 1) * CHUNK)
            for t in range(PACK):
                w_cols = slice(t * P, (t + 1) * P)
                nc.tensor.matmul_mx(
                    bank[:, t, :],
                    lhsT=wu_codes[a][:, w_cols].bitcast(FP8X4),
                    lhsT_scale=wu_scales[a][:, w_cols],
                    rhs=words_of(a, chunk).bitcast(FP8X4),
                    rhs_scale=v_scales[4 * a :, cols],
                    start=(a == 0 and t == 0),
                    stop=(a == PASSES - 1 and t == PACK - 1),
                )

        nc.vector.tensor_copy(v_scales[:], table_scales[:].indirect(offsets[:]))
        rounded = sb("wu_bf0", [P, PACK * R], BF16)
        slots_out = rounded[:].rearrange("p (t m j) -> p m j t", t=PACK, j=PACK)
        slots_in = wu_raw[0][:].rearrange("p j (m t) -> p m j t", t=PACK)
        nc.vector.tensor_copy(slots_out[:, :VECTOR_SHARE], slots_in[:, :VECTOR_SHARE])
        scalar_round(slots_out[:, VECTOR_SHARE:], slots_in[:, VECTOR_SHARE:])
        nc.vector.quantize_mx(wu_codes[0][:].bitcast(FP8X4), wu_scales[0][:], rounded[:])
        gather_words(0)
        banks = [psum.tile([P, PACK, CHUNK], F32, name="bank%d" % chunk) for chunk in range(UP_BANKS)]
        for chunk in range(UP_BANKS):
            up_pass(banks[chunk], 0, chunk)
        quantize_wu(1, (nc.vector.tensor_copy, scalar_round))
        spread = psum.tile([P, 2, P], F32, name="bank6")
        for c in range(2):
            at = 32 * c + 1
            nc.tensor.transpose(spread[:, c, :], bias_cols[:, at : at + 1].to_broadcast([P, P]), identity[:])
        gate_head = shared.tile([P, HEAD], F32, name="gate_head", offset=1024 - 2 * HEAD, align_bytes=64)
        nc.scalar.activation(gate_head[:], spread[:, 0, :HEAD], ACT.Copy)
        nc.scalar.activation(gate[:, : 2 * P], spread[:].rearrange("p c j -> p (c j)"), ACT.Copy)
        gate_first = {(0, HEAD): gate_head[:], (HEAD, 2 * P): gate[:, HEAD : 2 * P]}
        gather_words(1)

        def round_wd(name, raw, width, on=None, copy=scalar_round):
            rounded = sb(name, [P, PACK * width], BF16, on=on)
            copy(
                rounded[:].rearrange("p (c i j) -> p c j i", i=4, j=PACK),
                raw[:].rearrange("p j (c i) -> p c j i", i=4),
            )
            return rounded

        wd_codes, wd_scales = {}, {}

        def quantize_wd(c0, c1, rounded, on=None):
            codes = sb("wd_codes%d" % c0, [P, (c1 - c0) * P], U32, on=on)
            scales = sb("wd_scales%d" % c0, [P, (c1 - c0) * P], U8)
            nc.vector.quantize_mx(codes[:].bitcast(FP8X4), scales[:], rounded)
            for c in range(c0, c1):
                wd_codes[c] = codes[:, (c - c0) * P : (c - c0 + 1) * P]
                wd_scales[c] = scales[:, (c - c0) * P : (c - c0 + 1) * P]

        wd_first_bf = sb("wd_first_bf", [P, PACK * P], BF16)
        nc.gpsimd.tensor_copy(
            wd_first_bf[:].rearrange("p (n j) -> p n j", j=PACK)[:, :64],
            wd_first[:].rearrange("p j n -> p n j")[:, :64],
        )
        scalar_round(
            wd_first_bf[:, PACK * 64 :].rearrange("p (c i j) -> p c j i", i=4, j=PACK),
            wd_first[:, :, 64:].rearrange("p j (c i) -> p c j i", i=4),
        )

        h_bf = {lo: sb("h_bf%d" % lo, [P, PACK * (hi - lo)], BF16) for lo, hi in GROUPS}
        h_codes, h_scales = {}, {}

        def finish_up(lo, hi):
            for chunk in range(lo // CHUNK, hi // CHUNK):
                bank = banks[chunk]
                if chunk < 4:
                    up_pass(bank, 1, chunk)
                at = PACK * (CHUNK * chunk - lo)
                nc.scalar.activation(
                    h_bf[lo][:, at : at + PACK * CHUNK].rearrange("p (n t) -> p n t", t=PACK),
                    bank[:].rearrange("p t n -> p n t"),
                    ACT.Relu,
                )

        def quantize_h(lo, hi, on=None, scales=None):
            h_codes[lo] = sb("h_codes%d" % lo, [P, hi - lo], U32, on=on)
            h_scales[lo] = scales if scales is not None else sb("h_scales%d" % lo, [P, hi - lo], U8)
            nc.vector.quantize_mx(h_codes[lo][:].bitcast(FP8X4), h_scales[lo][:], h_bf[lo][:])

        down_count = []

        def down(c, groups, on=None):
            bank = psum.tile([P, 512], F32, name=on or "bank%d" % (len(down_count) % BANKS))
            down_count.append(c)
            at = 0
            for lo, hi in groups:
                nc.tensor.matmul_mx(
                    bank[:, at : at + hi - lo],
                    lhsT=wd_codes[c].bitcast(FP8X4),
                    lhsT_scale=wd_scales[c],
                    rhs=h_codes[lo][:].bitcast(FP8X4),
                    rhs_scale=h_scales[lo][:],
                    start=True,
                    stop=True,
                )
                at = at + hi - lo
            return bank[:, :at]

        def bias_of(c):
            return bias_cols[:, 32 * c : 32 * c + 1]

        def add_bias(dst, c, groups, on=None):
            nc.scalar.activation(dst, down(c, groups, on), ACT.Identity, bias=bias_of(c))

        def add_residual(c, lo, hi, y, on=None):
            total = sb("total%d_%d" % (c, lo), [P, hi - lo], F32, on=on)
            nc.vector.tensor_tensor(total[:], residual[c][:].indirect(listed(lo, hi)), y[:], ALU.add)
            return total

        def place(c, lo, hi, values):
            nc.vector.tensor_tensor(pages[c % 2][:].indirect(listed(lo, hi)), values[:], gate[:, lo:hi], ALU.mult)

        def store(c):
            nc.sync.dma_start(out[c * P : (c + 1) * P, :], pages[c % 2][:])

        finish_up(*first)
        finish_up(*second)
        up_pass(banks[4], 1, 4)
        up_pass(banks[5], 1, 5)
        quantize_wd(0, 1, wd_first_bf[:])
        quantize_h(*first)
        gated_residual = sb("gated_residual", [P, 256], F32)
        for (lo, hi), factor in gate_first.items():
            nc.vector.tensor_tensor(gated_residual[:, lo:hi], residual[0][:].indirect(listed(lo, hi)), factor, ALU.mult)
        gated_y = shared.tile([P, 256], F32, name="gated_y", offset=0, align_bytes=64)
        nc.vector.scalar_tensor_tensor(
            gated_y[:], down(0, [first], "bank7"), bias_of(0), gate[:, first[0] : first[1]], ALU.add, ALU.mult
        )
        for chunk in (6, 7):
            banks.append(psum.tile([P, PACK, CHUNK], F32, name="bank%d" % (chunk - 4)))
            up_pass(banks[chunk], 0, chunk)
            up_pass(banks[chunk], 1, chunk)
        second_scales = shared.tile([P, 256], U8, name="second_scales", offset=1024, align_bytes=64)
        quantize_h(*second, scales=second_scales)
        nc.vector.tensor_tensor(pages[0][:].indirect(listed(*first)), gated_residual[:], gated_y[:], ALU.add)
        y_second = sb("y_second", [P, second[1] - second[0]], F32)
        add_bias(y_second[:], 0, [second], "bank6")
        total_second = add_residual(0, *second, y_second)
        finish_up(*third)
        quantize_h(*third)
        quantize_wd(1, 2, round_wd("wd_second_bf", wd_second, P, on="wu_scales1")[:])
        place(0, *second, total_second)
        y_third = sb("y_third", [P, third[1] - third[0]], F32)
        add_bias(y_third[:], 0, [third], "bank0")
        waiting = (third, add_residual(0, *third, y_third))
        ys = {c: sb("y%d" % c, [P, J], F32) for c in range(1, BLOCKS)}
        add_bias(ys[1][:, : J // 2], 1, [first, second], "bank1")
        add_bias(ys[1][:, J // 2 :], 1, [third], "bank0")
        quantize_wd(2, BLOCKS, round_wd("wd_rest_bf", wd_rest, N - 2 * P, on="wu_codes1")[:], on="wd_codes1")
        place(0, *waiting[0], waiting[1])
        store(0)
        add_bias(ys[2][:, : J // 2], 2, [first, second], "bank4")
        add_bias(ys[2][:, J // 2 :], 2, [third], "bank5")
        add_bias(ys[3][:, : J // 2], 3, [first, second], "bank4")
        add_bias(ys[3][:, J // 2 :], 3, [third], "bank5")
        total = add_residual(1, 0, J, ys[1], on="wd_codes1")
        for c in range(1, BLOCKS):
            ahead = add_residual(c + 1, 0, J, ys[c + 1], on="h_codes512" if c == 1 else None) if c + 1 < BLOCKS else None
            place(c, 0, J, total)
            store(c)
            total = ahead
